import numpy as np, ml_dtypes
CORES = [3,11,19,27,35,43,51,59]
N = 8
BF = ml_dtypes.bfloat16
def gentries(a):
    return np.ascontiguousarray(a.reshape(8, 16, -1).transpose(0, 2, 1)).reshape(8, -1)
def gtable(e):
    e = np.asarray(e); return np.ascontiguousarray(e.reshape(8, -1, 16).transpose(0, 2, 1)).reshape(128, -1).astype(np.int32)
W, n, V, C, Z = 4, 4096, 16384, 1024, 256
def counts(rng, h, z):
    c = np.zeros((N, 8, W), np.int64)
    for r in range(N):
        for g in range(8):
            m = int(h[r, g] - z[r, g]) - (W - 2); b = np.sort(rng.integers(0, m + 1, W - 3))
            c[r, g, 0] = n - h[r, g]; c[r, g, 1:W - 1] = np.diff(np.concatenate([[0], b, [m]])) + 1; c[r, g, W - 1] = z[r, g]
    return c
def some(rng):
    return rng.integers(C - C // 4, C + 1, (N, 8)), rng.integers(Z // 2, Z + 1, (N, 8))
def names(rng):
    return np.stack([np.stack([rng.permutation(V)[:n] for g in range(8)]) for r in range(N)]).astype(np.int64)
def depths(rng, c):
    return np.stack([np.stack([rng.permutation(np.repeat(np.arange(W), c[r, g])) for g in range(8)]) for r in range(N)])
def link(rng, o, dep):
    x = np.zeros((N, 8, n), np.int64)
    for r in range(N):
        q = (r + 1) % N
        for g in range(8):
            m = np.ones(V, bool); m[o[q, g]] = False; free = np.flatnonzero(m)
            v = free[rng.integers(0, len(free), n)]
            for k in range(1, W):
                i = np.flatnonzero(dep[r, g] == k)
                if len(i):
                    t = np.flatnonzero(dep[q, g] == k - 1 if k < W - 1 else dep[q, g] >= W - 2)
                    v[i] = o[q, g][t[rng.integers(0, len(t), len(i))]]
            x[r, g] = v
    return x
def pack(o, x, s):
    return {"own": np.stack([gtable(a) for a in o]), "nxt": np.stack([gtable(a) for a in x]), "pts": np.asarray(s).astype(np.int32)}
def points(rng):
    return rng.integers(0, 256, (N, 8, n))
def setup_inputs(rng):
    h, z = some(rng); o = names(rng); dep = depths(rng, counts(rng, h, z))
    return pack(o, link(rng, o, dep), points(rng))
def setup_inputs_full(rng):
    o = names(rng); c = counts(rng, np.full((N, 8), C), np.full((N, 8), Z)); e = rng.permutation(8)[:4]
    c[:, e, 1:W - 2] = 1; c[:, e, W - 2] = C - Z - (W - 3)
    dep = depths(rng, c)
    return pack(o, link(rng, o, dep), points(rng))
def setup_inputs_few(rng):
    h, z = some(rng); e = rng.permutation(8); q = int(rng.integers(0, N)); o = names(rng)
    z[:, e[2]] = 1; z[:, e[3]] = np.where(rng.random(N) < 0.5, 0, z[:, e[3]]); z[q, e[3]] = 0; z[:, e[4]] = Z; h[:, e[4]] = C
    c = counts(rng, h, z); c[:, e[0], 0] = n; c[:, e[0], 1:] = 0
    for t in range(W - 1):
        r = (q - t) % N; c[r, e[1], 0] += np.sum(c[r, e[1], t + 1:]); c[r, e[1], t + 1:] = 0
    dep = depths(rng, c)
    return pack(o, link(rng, o, dep), points(rng))
def setup_inputs_repeats(rng):
    h, z = some(rng); o = names(rng); dep = depths(rng, counts(rng, h, z)); x = link(rng, o, dep)
    for r in range(N):
        for g in range(8):
            for k in (0, W - 1):
                i = np.flatnonzero(dep[r, g] == k); x[r, g, i] = x[r, g, i[0]]
    return pack(o, x, points(rng))
def setup_inputs_ends(rng):
    h, z = some(rng); dep = depths(rng, counts(rng, h, z))
    o = 1 + np.stack([np.stack([rng.permutation(V - 2)[:n] for g in range(8)]) for r in range(N)]).astype(np.int64)
    for r in range(N):
        for g in range(0, 8, 2):
            o[r, g, 0] = 0; o[r, g, n - 1] = V - 1; a = dep[r, g]
            i = np.flatnonzero(a == W - 1); j = i[rng.integers(0, len(i))]; u, v = int(a[0]), int(a[j]); a[j] = u; a[0] = v
            i = np.flatnonzero(a[1:] == W - 1) + 1; j = i[rng.integers(0, len(i))]; u, v = int(a[n - 1]), int(a[j]); a[j] = u; a[n - 1] = v
    x = link(rng, o, dep)
    x[:, 0::2, 0] = V - 1; x[:, 0::2, n - 1] = 0
    for g in range(1, 8, 2):
        m = (dep[:, g] == 0) & (rng.random((N, n)) < 0.5)
        x[:, g] = np.where(m, rng.integers(0, 2, (N, n)) * (V - 1), x[:, g])
    return pack(o, x, 255 * rng.integers(0, 2, (N, 8, n)))
def setup_inputs_spread(rng):
    z = np.maximum(Z >> rng.integers(0, 7, (N, 8)), 1); h = z + np.maximum((C - Z) >> rng.integers(0, 7, (N, 8)), W - 2)
    o = np.stack([np.stack([(rng.integers(0, V) + rng.permutation(n + n // 8)[:n]) % V for g in range(8)]) for r in range(N)]).astype(np.int64)
    o[:, 1::2] = np.sort(o[:, 1::2], axis=2)
    dep = depths(rng, counts(rng, h, z))
    return pack(o, link(rng, o, dep), 255 >> rng.integers(0, 9, (N, 8, n)))
def followers(o, x):
    to = np.zeros((N, 8, n), np.int64)
    for r in range(N):
        for g in range(8):
            where = np.full(V, -1, np.int64); where[o[(r + 1) % N, g]] = np.arange(n); to[r, g] = where[x[r, g]]
    return to
def step(p, v, t):
    return np.take_along_axis(np.roll(v, -t, axis=0), p, axis=2)
def chains(to, s):
    p = np.broadcast_to(np.arange(n), (N, 8, n)); tot = s.astype(np.int64)
    for t in range(1, W):
        p = np.where(p >= 0, step(np.maximum(p, 0), to, t - 1), -1)
        tot = tot + np.where(p >= 0, step(np.maximum(p, 0), s, t), 0)
    return p, tot
def check_inputs(d):
    try:
        o = np.stack([gentries(a) for a in d["own"]]).astype(np.int64); x = np.stack([gentries(a) for a in d["nxt"]]).astype(np.int64); s = np.asarray(d["pts"]).astype(np.int64)
        if o.shape != (N, 8, n) or x.shape != (N, 8, n) or s.shape != (N, 8, n): return ["shapes"]
        bad = []
        if s.min() < 0 or s.max() > 255: bad.append("points")
        if o.min() < 0 or o.max() >= V or x.min() < 0 or x.max() >= V: return bad + ["names in range"]
        if (np.diff(np.sort(o, axis=2), axis=2) == 0).any(): return bad + ["own names differ"]
        to = followers(o, x); p, tot = chains(to, s)
        if np.max(np.count_nonzero(to >= 0, axis=2)) > C: bad.append("followers")
        if np.max(np.count_nonzero(p >= 0, axis=2)) > Z: bad.append("kept")
        return bad
    except Exception:
        return ["shapes"]
def reference(own, nxt, pts):
    o = np.stack([gentries(a) for a in own]).astype(np.int64); x = np.stack([gentries(a) for a in nxt]).astype(np.int64)
    p, tot = chains(followers(o, x), pts)
    yk = np.full((N, 8, Z), -1, np.float32); ys = np.zeros((N, 8, Z), np.float32)
    for r in range(N):
        for g in range(8):
            i = np.flatnonzero(p[r, g] >= 0)
            yk[r, g, :len(i)] = o[r, g, i]; ys[r, g, :len(i)] = tot[r, g, i]
    return {"yk": yk, "ys": ys}

@@ -1,0 +1,419 @@
+from concourse.bass import DstId, RemoteDMATransfer
+from concourse.mybir import AluOpType as A, ActivationFunctionType as F
+
+BF, F32, F16, I32, U16 = "bfloat16", "float32", "float16", "int32", "uint16"
+SCRATCH = {
+    "own_i": ("sbuf", [128, 256], I32), "nxt_i": ("sbuf", [128, 256], I32), "pts_i": ("sbuf", [128, 256], I32),
+    "own_u": ("sbuf", [128, 256], U16), "nxt_u": ("sbuf", [128, 256], U16), "own_r": ("sbuf", [128, 256], U16),
+    "own_f": ("sbuf", [128, 256], F32), "ptsb": ("sbuf", [128, 256], BF), "zb": ("sbuf", [128, 2048], BF),
+    "tab": ("sbuf", [128, 16384], BF), "dat": ("sbuf", [128, 4096], BF), "gat": ("sbuf", [128, 4096], BF),
+    "pidx": ("sbuf", [128, 1], I32), "par": ("sbuf", [128, 1], I32), "p16": ("sbuf", [128, 1], I32),
+    "colA": ("sbuf", [128, 1], F32), "colB": ("sbuf", [128, 1], F32), "colF": ("sbuf", [128, 1], F32),
+    "colW": ("sbuf", [128, 1], F32), "lb0": ("sbuf", [128, 8], F32), "lb": ("sbuf", [128, 8], F32),
+    "bl": ("sbuf", [128, 256], BF), "bh": ("sbuf", [128, 256], BF), "bx": ("sbuf", [128, 256], BF),
+    "by": ("sbuf", [128, 256], BF), "bs": ("sbuf", [128, 256], BF),
+    "cz": ("sbuf", [128, 1760], BF), "cf": ("sbuf", [128, 384], F32),
+    "z1": ("sbuf", [128, 144], F16), "ones": ("sbuf", [1, 128], BF),
+    "rc1": ("sbuf", [1, 512], BF), "rc2": ("sbuf", [1, 512], BF),
+    "mrow": ("sbuf", [128, 1024], F32), "cio": ("sbuf", [128, 512], F32), "rw": ("sbuf", [128, 64], F32),
+    "mk": ("sbuf", [128, 1536], F32), "oxf": ("sbuf", [128, 1024], F32),
+    "pr8": ("sbuf", [8, 4096], BF), "pt": ("sbuf", [128, 256], BF), "npt": ("sbuf", [128, 512], F32),
+    "hl": ("sbuf", [128, 512], BF), "hp": ("sbuf", [128, 256], BF), "fl": ("sbuf", [128, 528], BF),
+    "ax": ("sbuf", [128, 512], F32), "o16": ("sbuf", [128, 512], F16), "wq": ("sbuf", [128, 512], F32),
+    "ol": ("sbuf", [128, 32], U16), "cm": ("sbuf", [128, 1024], F16), "l1": ("sbuf", [128, 64], U16),
+    "sel": ("sbuf", [128, 1024], BF), "hls": ("sbuf", [128, 1024], BF), "nps": ("sbuf", [128, 1024], F32),
+    "l2": ("sbuf", [128, 64], U16), "l3": ("sbuf", [128, 64], U16), "l4": ("sbuf", [128, 64], U16),
+    "tb1": ("sbuf", [128, 4112], BF), "tb2": ("sbuf", [128, 4112], BF),
+    "r1": ("sbuf", [128, 1024], BF), "r2": ("sbuf", [128, 1024], BF),
+    "fl4": ("sbuf", [128, 72], BF), "xn": ("sbuf", [128, 64], F32), "xx": ("sbuf", [128, 64], F32),
+    "a4": ("sbuf", [128, 64], F32), "q4": ("sbuf", [128, 64], F32), "o4": ("sbuf", [128, 64], F32),
+    "fd": ("sbuf", [128, 1024], F32), "win": ("sbuf", [128, 1408], F32),
+    "landp": ("dram", [128, 256], BF), "pd": ("dram", [128, 256], BF),
+    "lpt1": ("dram", [128, 256], BF), "lpt2": ("dram", [128, 256], BF), "lhp": ("dram", [128, 256], BF),
+    "lhl1": ("dram", [128, 512], BF), "lhl2": ("dram", [128, 512], BF),
+}
+for _b in range(8):
+    SCRATCH["ps%d" % _b] = ("psum", [128, 512], F32)
+NE = 138
+SEMAPHORES = ["own_r_s", "landp_s", "lpt1_s", "lpt2_s", "lhl1_s", "lhl2_s", "lhp_s", "ls"] + ["e%d" % _i for _i in range(NE)]
+
+ZS, ZW, ZC, ZP, EP, Z1, OC, ON4, TC, DG, FO, FT, FP = 0, 144, 288, 432, 576, 720, 864, 992, 1120, 1248, 1376, 1504, 1632
+
+
+def rank_program(g, core, T, topo):
+    r = T.rank_of(core)
+    if r is None:
+        return
+    n = len(T.cores)
+    d1, d2 = T.cores[(r - 1) % n], T.cores[(r - 2) % n]
+    s1, s2 = T.cores[(r + 1) % n], T.cores[(r + 2) % n]
+    V, S, P, Y = g.vector, g.scalar, g.tensor, g.sync
+    Q = {"g": g, "v": V, "s": S, "p": P, "y": Y}
+    ctr, seen, waited, made, ls = [0], {}, {}, [], [0]
+
+    def new():
+        t = ["e%d" % ctr[0], 0]
+        ctr[0] += 1
+        made.append(t)
+        return t
+
+    def sig(ins, t=None, by=1):
+        t = t or new()
+        ins.then_inc(T.sem[t[0]], by)
+        t[1] += by
+        return t
+
+    def dsig(ins, t=None):
+        return sig(ins, t, 16)
+
+    def w(q, *toks):
+        for t in toks:
+            if seen.get((q, t[0]), 0) < t[1]:
+                Q[q].wait_ge(T.sem[t[0]], t[1])
+                seen[(q, t[0])] = t[1]
+                waited[t[0]] = t[1]
+
+    def landed(q, nm, cnt):
+        Q[q].wait_ge(T.sem[nm], cnt)
+
+    def send(dst, out, in_, sem):
+        rid, pid = topo.addr(dst)[:2]
+        g.remote_dma(out_ap=out, in_ap=in_, remote_sem=T.sem[sem], local_sem=T.sem.ls, pid=pid, routing_id=rid,
+                     dma_engine_mask=topo.mask(core, dst))
+        ls[0] += len(topo.engines(core, dst))
+
+    def iota(out, pattern, base=0, cm=0):
+        return g.iota(out, pattern, base, cm, allow_small_or_imprecise_dtypes=True)
+
+    def cz(b, width=128, rows=128):
+        return T.cz[0:rows, b:b + width]
+
+    def mm(out, lhsT, rhs, first, last):
+        return P.matmul(out, lhsT, rhs, first, last)
+
+    ps = [T["ps%d" % b] for b in range(8)]
+    n1, n2 = len(topo.engines(s1, core)), len(topo.engines(s2, core))
+    nh = n1 // 2
+
+    t_own = dsig(Y.dma_start(T.own_i[:, :], T.own[:, :]))
+    t_pts = dsig(S.dma_start(T.pts_i[:, :], T.pts[:, :]))
+    t_nxt = dsig(Y.dma_start(T.nxt_i[:, :], T.nxt[:, :]))
+
+    k0 = new()
+    sig(g.iota(T.pidx[:, :], [[0, 1]], 0, 1), k0)
+    sig(iota(T.lb0[:, :], [[32, 8]]), k0)
+    sig(iota(T.bl[:, :], [[1, 32], [0, 8]]), k0)
+    sig(iota(T.bh[:, :], [[0, 32], [2, 8]]), k0)
+
+    z0 = sig(V.memset(T.zb[:, :], 0.0))
+    w("s", z0)
+    f_tab = new()
+    for a in range(8192, 16384, 2048):
+        sig(S.activation(T.tab[:, a:a + 2048], T.zb[:, :], F.Copy), f_tab)
+
+    w("v", k0)
+    c1 = new()
+    sig(V.tensor_scalar(T.par[:, :], T.pidx[:, :], 1, None, A.bitwise_and), c1)
+    sig(V.tensor_scalar(T.p16[:, :], T.pidx[:, :], 15, None, A.bitwise_and), c1)
+    w("v", c1)
+    cc = new()
+    sig(V.tensor_copy(T.colB[:, :], T.par[:, :]), cc)
+    sig(V.tensor_scalar(T.colA[:, :], T.par[:, :], 0, None, A.is_equal), cc)
+    sig(V.tensor_scalar(T.colF[:, :], T.p16[:, :], 0, -1.0, A.is_equal, A.mult), cc)
+    sig(V.tensor_scalar(T.colW[:, :], T.par[:, :], -255.0, 256.0, A.mult, A.add), cc)
+    w("v", cc)
+    b1 = new()
+    sig(V.tensor_scalar(T.lb[:, :], T.lb0[:, :], T.colB[:, :], None, A.mult), b1)
+    sig(V.tensor_scalar(T.bx[:, :], T.bl[:, :], T.colB[:, :], 1.0, A.mult, A.add), b1)
+    sig(V.tensor_scalar(T.by[:, :], T.bh[:, :], T.colA[:, :], None, A.mult), b1)
+    w("v", b1)
+    b2 = sig(V.tensor_tensor(T.bs[:, :], T.bx[:, :], T.by[:, :], A.add))
+    w("v", t_own)
+    c_own = sig(V.tensor_copy(T.own_u[:, :], T.own_i[:, :]))
+    w("v", t_pts)
+    c_pts = sig(V.tensor_copy(T.ptsb[:, :], T.pts_i[:, :]))
+
+    w("g", c_own, c_pts)
+    rid, pid = topo.addr(d1)[:2]
+    eng = topo.engines(core, d1)
+    h = len(eng) // 2
+    g.remote_dma_fused([
+        RemoteDMATransfer(srcs=[T.ptsb[:, :]], dsts=[T.landp[:, :]], dst_ids=[DstId(rid=rid, pnc=pid)],
+                          dma_engine_mask=sum(1 << e for e in eng[:h]), remote_sem=T.sem.landp_s),
+        RemoteDMATransfer(srcs=[T.own_u[:, :]], dsts=[T.own_r[:, :]], dst_ids=[DstId(rid=rid, pnc=pid)],
+                          dma_engine_mask=sum(1 << e for e in eng[h:2 * h]), remote_sem=T.sem.own_r_s)],
+        local_sem=T.sem.ls)
+    ls[0] += 2 * h
+
+    w("v", b2)
+    dd = new()
+    for ch in range(8):
+        sig(V.tensor_scalar(T.dat[:, 256 * ch:256 * ch + 256], T.bs[:, :], T.lb[:, ch:ch + 1], None, A.add), dd)
+    w("v", dd)
+    dd2 = sig(V.tensor_scalar(T.dat[:, 2048:4096], T.dat[:, 0:2048], T.colA[:, :], None, A.add))
+    w("y", c_pts)
+    t_pd = dsig(Y.dma_start(T.pd[:, :], T.ptsb[:, :]))
+    w("y", t_pd)
+    t_pr8 = dsig(Y.dma_start(T.pr8[:, :], T.pd[:, :]))
+    w("y", dd, dd2)
+    landed("y", "landp_s", nh)
+    t_dat = dsig(Y.dma_start(T.dat[2:128:16, :], T.landp[:, :]))
+    w("v", t_nxt)
+    c_nxt = sig(V.tensor_copy(T.nxt_u[:, :], T.nxt_i[:, :]))
+    c_ownf = sig(V.tensor_copy(T.own_f[:, :], T.own_i[:, :]))
+    f_tabv = sig(V.memset(T.tab[:, 0:8192], 0.0))
+    zz = new()
+    sig(V.memset(T.fl[:, 0:8], 0.0), zz)
+    sig(V.memset(T.fl4[:, 0:8], 0.0), zz)
+
+    w("v", f_tabv, f_tab, dd, dd2, t_dat)
+    landed("v", "own_r_s", nh)
+    t_sc = sig(V.tensor_copy(T.tab[:, :].indirect(T.own_r[:, :]), T.dat[:, :]))
+
+    w("y", z0)
+    t_tb = new()
+    for tb in (T.tb1, T.tb2):
+        for a, b in ((0, 2048), (2048, 4096), (4096, 4112)):
+            dsig(Y.dma_start(tb[:, a:b], T.zb[:, 0:b - a]), t_tb)
+
+    k1 = new()
+    sig(iota(T.cz[:, :], [[0, 1760]]), k1)
+    sig(iota(T.cf[:, :], [[0, 384]]), k1)
+    sig(iota(T.ones[:, :], [[0, 128]], 1), k1)
+    w("g", k1)
+
+    def view(b, start):
+        return T.cz[:, b + start:b + start + 113:16]
+
+    def one(b, start, part, wt):
+        return g.affine_select(view(b, start), view(b, start), [[-16, 8]], A.not_equal, wt, -part, 1)
+
+    def setw(x, pattern, wt, base, cm):
+        return g.affine_select(x, x, pattern, A.is_ge, wt, base, cm)
+    k2 = new()
+    ep = T.cz[0:8, EP + 15:EP + 128:16]
+    sig(g.affine_select(ep, ep, [[-1, 8]], A.not_equal, 1.0, 0, 1), k2)
+    for hh in range(2):
+        na = T.cf[:, 128 * hh:128 * hh + 128:2]
+        sig(g.affine_select(na, na, [[-16, 8], [-1, 8]], A.not_equal, 1.0, -8 * hh, 1), k2)
+    sig(one(ZS, 14, 0, 1.0), k2)
+    sig(one(ZS, 15, 1, 1.0), k2)
+    sig(one(ZP, 15, 2, 1.0), k2)
+    sig(one(Z1, 15, 0, 1.0), k2)
+    grp = [[16, 8], [0, 16]]
+    vz, ve, vo = view(ZC, 15), T.cf[:, 256:384:16], T.cf[:, 257:384:16]
+    k3, k4 = new(), new()
+    for b, wt in ((OC, 0.5), (ON4, -2048.0), (TC, 0.5), (FO, 1.0), (FT, 1.0)):
+        sig(setw(cz(b), grp, wt, -1, -1), k3)
+    sig(g.affine_select(cz(DG), cz(DG), [[-1, 128]], A.not_equal, 2048.0, 0, 1), k3)
+    sig(one(ZW, 15, 0, 256.0), k3)
+    sig(one(FP, 1, 2, 1.0), k3)
+    for x in (vz, ve, vo):
+        sig(setw(x, [[16, 8]], 1.0, -1, -1), k3)
+    w("g", k3)
+    for b in (OC, ON4, FO):
+        sig(setw(cz(b), grp, 0.0, 15, -1), k4)
+    sig(setw(cz(TC), [[16, 8], [2, 8], [0, 2]], 0.0, 1, -1), k4)
+    sig(setw(cz(FT), [[1, 128]], 0.0, 0, -1), k4)
+    sig(one(ZW, 15, 1, 1.0), k4)
+    sig(one(FP, 1, 3, 1.0), k4)
+    for x in (vz, ve, vo):
+        sig(setw(x, [[16, 8]], 0.0, 15, -1), k4)
+    k5 = new()
+    sig(iota(T.rc1[:, :], [[8, 64], [0, 8]], 1024), k5)
+    sig(iota(T.rc2[:, :], [[0, 64], [1, 8]]), k5)
+    sig(iota(T.cio[:, :], [[1, 512]]), k5)
+    sig(iota(T.mrow[:, :], [[1, 1024]], 2049), k5)
+    sig(iota(T.rw[:, :], [[16, 64]], 264, 1), k5)
+
+    fo, fm = new(), new()
+    sig(S.activation(T.oxf[:, 0:1024], T.zb[:, 0:1024], F.Copy), fo)
+    w("s", fo, c_ownf, cc)
+    ox = new()
+    sig(S.activation(T.oxf[:, 0:512:2], T.own_f[:, :], F.Copy), ox)
+    sig(S.activation(T.oxf[:, 513:1024:2], T.own_f[:, :], F.Copy), ox)
+    sig(S.activation(T.mk[:, 0:1024], T.zb[:, 0:1024], F.Copy), fm)
+    sig(S.activation(T.win[:, 0:264], T.zb[:, 0:264], F.Identity, bias=T.colF[:, :]), fm)
+    w("p", t_pr8, k2)
+    for kk in range(16):
+        k, hh = kk // 2, kk % 2
+        m = mm(ps[2][:, 0:256], cz(EP + 15 - kk, 128, 8), T.pr8[:, hh * 2048 + k:hh * 2048 + 2048:8], kk == 0, kk == 15)
+    m_pt = sig(m)
+    w("p", ox)
+    for hh in range(2):
+        mm(ps[3][:, :], T.cf[:, 128 * hh:128 * hh + 128], T.oxf[:, 512 * hh:512 * hh + 512], hh == 0, False)
+    for k in range(8):
+        m = mm(ps[3][:, :], cz(EP + 14 - 2 * k, 128, 8), T.pr8[:, k:4096:8], False, k == 7)
+    m_np = sig(m)
+    w("s", m_pt)
+    c_pt = sig(S.activation(T.pt[:, :], ps[2][:, 0:256], F.Copy))
+    w("s", m_np)
+    c_np = sig(S.activation(T.npt[:, :], ps[3][:, :], F.Copy))
+    w("s", k4)
+    ksc = new()
+    sig(S.activation(vz, vz, F.Copy, scale=T.colW[:, :]), ksc)
+    sig(S.activation(ve, ve, F.Copy, scale=T.colA[:, :]), ksc)
+    sig(S.activation(vo, vo, F.Copy, scale=T.colB[:, :]), ksc)
+    w("g", c_pt)
+    send(d1, T.lpt1[:, :], T.pt[:, :], "lpt1_s")
+    send(d2, T.lpt2[:, :], T.pt[:, :], "lpt2_s")
+    w("y", t_tb)
+    tab1, tab2 = new(), new()
+    landed("y", "lpt1_s", n1)
+    dsig(Y.dma_start(T.tb1[2:128:16, 16:4112], T.lpt1[:, :]), tab1)
+    landed("y", "lpt2_s", n2)
+    dsig(Y.dma_start(T.tb2[2:128:16, 16:4112], T.lpt2[:, :]), tab2)
+
+    w("s", t_sc, c_nxt)
+    w("v", t_sc, c_nxt)
+    gt = [None] * 4
+    for i in range(2):
+        for j in (i, i + 2):
+            o, src = T.gat[:, 1024 * j:1024 * j + 1024], T.tab[:, :].indirect(T.nxt_u[:, 64 * j:64 * j + 64])
+            gt[j] = sig(V.tensor_copy(o, src) if j < 2 else S.activation(o, src, F.Copy))
+    m_hl = [new(), new()]
+    for j in (0, 2, 1, 3):
+        w("p", gt[j])
+        b, c0 = j // 2, 128 * (j % 2)
+        for k in range(8):
+            m = mm(ps[b][:, c0:c0 + 128], cz(ZS + 14 - 2 * k), T.gat[:, 1024 * j + k:1024 * j + 1024:8], k == 0, k == 7)
+        sig(m, m_hl[b])
+    w("v", m_hl[0])
+    hla = sig(V.tensor_copy(T.hl[:, 0:256], ps[0][:, 0:256]))
+    w("s", m_hl[1])
+    hlb = sig(S.activation(T.hl[:, 256:512], ps[1][:, 0:256], F.Copy))
+    w("g", hla, hlb)
+    send(d1, T.lhl1[:, :], T.hl[:, :], "lhl1_s")
+    send(d2, T.lhl2[:, :], T.hl[:, :], "lhl2_s")
+    landed("y", "lhl1_s", n1)
+    dsig(Y.dma_start(T.tb1[0:128:16, 16:4112], T.lhl1[0:128:2, :]), tab1)
+    dsig(Y.dma_start(T.tb1[1:128:16, 16:4112], T.lhl1[1:128:2, :]), tab1)
+    landed("y", "lhl2_s", n2)
+    dsig(Y.dma_start(T.tb2[0:128:16, 16:4112], T.lhl2[0:128:2, :]), tab2)
+    dsig(Y.dma_start(T.tb2[1:128:16, 16:4112], T.lhl2[1:128:2, :]), tab2)
+
+    w("v", hla, hlb, zz)
+    fl = sig(V.tensor_scalar(T.fl[:, 8:520], T.hl[:, :], 0.0, None, A.is_gt))
+    w("v", k2)
+    z1h = sig(V.tensor_copy(T.z1[:, :], cz(Z1, 144)))
+    flx, fls = T.fl[:, 8:520], T.fl[:, 7:519]
+    w("p", fl, zz, k3, k4, c_pt)
+    m_c = sig(mm(ps[2][:, :], cz(OC), fls, True, True))
+    w("p", k1, k5, c_np)
+    mm(ps[3][:, :], cz(ON4), flx, True, False)
+    mm(ps[3][:, :], T.ones[:, :], T.rc1[:, :], False, False)
+    m_x = sig(mm(ps[3][:, :], T.ones[:, :], T.rc2[:, :], False, True))
+
+    def hp(lo, hi):
+        m = None
+        for kk in range(lo, hi):
+            k, hh = kk // 2, kk % 2
+            m = mm(ps[0][:, 0:256], cz(ZP + 15 - kk), T.gat[:, hh * 2048 + k:hh * 2048 + 2048:8], kk == 0, kk == 15)
+        return m
+    w("p", hla)
+    hp(0, 4)
+    w("v", m_c, z0)
+    ta = sig(V.tensor_tensor_scan(T.ax[:, :], ps[2][:, :], T.zb[:, 0:512], 0.0, A.add, A.add))
+    w("v", ta, m_x)
+    to = sig(V.tensor_tensor(T.o16[:, :], T.ax[:, :], ps[3][:, :], A.max))
+    w("p", to, z1h)
+    for k in range(16):
+        m = mm(ps[5][:, 0:32], T.z1[:, 15 - k:143 - k], T.o16[:, k:512:16], k == 0, k == 15)
+    m_o = sig(m)
+    mm(ps[4][:, :], cz(TC), flx, True, False)
+    m_p = sig(mm(ps[4][:, :], cz(DG), flx, False, True))
+    m_hp = sig(hp(4, 16))
+    w("v", m_o)
+    tol = sig(V.tensor_copy(T.ol[:, :], ps[5][:, 0:32]))
+    w("v", tol, fm, k5)
+    tmk = sig(V.tensor_copy(T.mk[:, :].indirect(T.ol[:, :]), T.cio[:, :]))
+    w("v", m_p)
+    twq = sig(V.tensor_tensor(T.wq[:, :], T.ax[:, :], ps[4][:, :], A.add))
+    w("v", tmk)
+    tcm = sig(V.tensor_tensor_scan(T.cm[:, :], T.mk[:, 0:1024], T.zb[:, 0:1024], 0.0, A.max, A.max))
+    w("s", m_hp)
+    c_hp = sig(S.activation(T.hp[:, :], ps[0][:, 0:256], F.Copy))
+    w("g", c_hp)
+    send(d2, T.lhp[:, :], T.hp[:, :], "lhp_s")
+    landed("y", "lhp_s", n2)
+    dsig(Y.dma_start(T.tb2[3:128:16, 16:4112], T.lhp[:, :]), tab2)
+    w("p", tcm)
+    for k in range(16):
+        m = mm(ps[5][:, 64:128], T.z1[:, 15 - k:143 - k], T.cm[:, k:1024:16], k == 0, k == 15)
+    m_l1 = sig(m)
+    w("v", m_l1)
+    tl1 = sig(V.tensor_copy(T.l1[:, :], ps[5][:, 64:128]))
+    w("v", tl1, twq)
+    tse = sig(V.tensor_tensor(T.sel[:, :], T.wq[:, :].indirect(T.l1[:, :]), T.mrow[:, :], A.is_equal))
+    w("v", tse)
+    ths = sig(V.tensor_tensor(T.hls[:, :], T.hl[:, :].indirect(T.l1[:, :]), T.sel[:, :], A.mult))
+    w("p", ths, ksc)
+    for k in range(16):
+        m = mm(ps[5][:, 128:192], cz(ZC + 15 - k), T.hls[:, k:1024:16], k == 0, k == 15)
+    m_l2 = sig(m)
+    w("v", c_np)
+    tnp = []
+    for hh in range(2):
+        sl = slice(512 * hh, 512 * hh + 512)
+        tnp.append(sig(V.tensor_tensor(T.nps[:, sl], T.npt[:, :].indirect(T.l1[:, 32 * hh:32 * hh + 32]), T.sel[:, sl], A.mult)))
+        if hh == 0:
+            w("v", m_l2)
+            tl2 = sig(V.tensor_scalar(T.l2[:, :], ps[5][:, 128:192], -241.0, None, A.add))
+    for hh in range(2):
+        w("p", tnp[hh])
+        mm(ps[6 + hh][:, :], T.cf[:, 256:384], T.nps[:, 512 * hh:512 * hh + 512], True, False)
+
+    def pick(tb, lst, out, toks):
+        ts = []
+        for q, sl, ll in (("v", slice(0, 512), slice(0, 32)), ("s", slice(512, 1024), slice(32, 64))):
+            w(q, *toks)
+            src = tb[:, :].indirect(lst[:, ll])
+            ts.append(sig(V.tensor_copy(out[:, sl], src) if q == "v" else S.activation(out[:, sl], src, F.Copy)))
+        return ts
+    tr1 = pick(T.tb1, T.l2, T.r1, [tl2, tab1])
+    w("p", hlb, *tr1)
+    for k in range(16):
+        m = mm(ps[1][:, 0:64], cz(ZW + 15 - k), T.r1[:, k:1024:16], k == 0, k == 15)
+    m_l3 = sig(m)
+    for hh in range(2):
+        mm(ps[6 + hh][:, :], cz(FP), T.r1[:, 512 * hh:512 * hh + 512], False, False)
+    w("v", m_l3)
+    tl3 = sig(V.tensor_scalar(T.l3[:, :], ps[1][:, 0:64], -241.0, None, A.add))
+    tr2 = pick(T.tb2, T.l3, T.r2, [tl3, tab2])
+    w("p", *tr2)
+    for k in range(16):
+        m = mm(ps[1][:, 64:128], cz(ZW + 15 - k), T.r2[:, k:1024:16], k == 0, k == 15)
+    m_l4 = sig(m)
+    m_fd = [sig(mm(ps[6 + hh][:, :], cz(FP), T.r2[:, 512 * hh:512 * hh + 512], False, True)) for hh in range(2)]
+
+    w("v", m_l4)
+    f4 = sig(V.tensor_scalar(T.fl4[:, 8:72], ps[1][:, 64:128], 0.0, None, A.is_gt))
+    x1 = sig(V.tensor_scalar(T.xn[:, :], ps[1][:, 64:128], 0.0, -4096.0, A.is_gt, A.mult))
+    w("p", f4)
+    m_a = sig(mm(ps[2][:, 0:64], cz(FO), T.fl4[:, 7:71], True, True))
+    m_q = sig(mm(ps[3][:, 0:64], cz(FT), T.fl4[:, 8:72], True, True))
+    w("v", x1)
+    x2 = sig(V.tensor_tensor(T.xx[:, :], T.xn[:, :], T.rw[:, :], A.add))
+    tfd = []
+    for hh in range(2):
+        w("s", m_fd[hh])
+        tfd.append(sig(S.activation(T.fd[:, 512 * hh:512 * hh + 512], ps[6 + hh][:, :], F.Copy)))
+    w("v", m_a)
+    q1 = sig(V.tensor_tensor_scan(T.a4[:, :], ps[2][:, 0:64], T.zb[:, 0:64], 0.0, A.add, A.add))
+    w("v", q1, m_q)
+    q2 = sig(V.tensor_tensor(T.q4[:, :], T.a4[:, :], ps[3][:, 0:64], A.add))
+    w("v", q2, x2)
+    q3 = sig(V.tensor_tensor(T.o4[:, :], T.q4[:, :], T.xx[:, :], A.max))
+    w("v", q3)
+    q5 = sig(V.tensor_copy(T.l4[:, :], T.o4[:, :]))
+    w("v", q5, *tfd)
+    tw = sig(V.tensor_copy(T.win[:, :].indirect(T.l4[:, :]), T.fd[:, :]))
+    w("y", tw)
+    t_y = new()
+    w("s", tw)
+    dsig(Y.dma_start(T.yk[:, :], T.win[0:128:16, 1:257]), t_y)
+    dsig(S.dma_start(T.ys[:, :], T.win[1:128:16, 1:257]), t_y)
+    for t in made:
+        if waited.get(t[0], 0) < t[1]:
+            w("y", t)
+    g.wait_ge(T.sem.ls, ls[0])

@@ -1,34 +1,37 @@
-from concourse.bass import DstId, RemoteDMATransfer
 from concourse.mybir import AluOpType as A, ActivationFunctionType as F
 
 BF, F32, F16, I32, U16 = "bfloat16", "float32", "float16", "int32", "uint16"
 SCRATCH = {
     "own_i": ("sbuf", [128, 256], I32), "nxt_i": ("sbuf", [128, 256], I32), "pts_i": ("sbuf", [128, 256], I32),
     "own_u": ("sbuf", [128, 256], U16), "nxt_u": ("sbuf", [128, 256], U16), "own_r": ("sbuf", [128, 256], U16),
-    "own_f": ("sbuf", [128, 256], F32), "ptsb": ("sbuf", [128, 256], BF), "zb": ("sbuf", [128, 2048], BF),
+    "onh": ("sbuf", [128, 256], I32), "onl": ("sbuf", [128, 256], I32), "nmb": ("sbuf", [128, 512], BF),
+    "ptsb": ("sbuf", [128, 256], BF), "zb": ("sbuf", [128, 2048], BF),
     "tab": ("sbuf", [128, 16384], BF), "dat": ("sbuf", [128, 4096], BF), "gat": ("sbuf", [128, 4096], BF),
     "pidx": ("sbuf", [128, 1], I32), "par": ("sbuf", [128, 1], I32), "p16": ("sbuf", [128, 1], I32),
     "colA": ("sbuf", [128, 1], F32), "colB": ("sbuf", [128, 1], F32), "colF": ("sbuf", [128, 1], F32),
-    "colW": ("sbuf", [128, 1], F32), "lb0": ("sbuf", [128, 8], F32), "lb": ("sbuf", [128, 8], F32),
+    "colU": ("sbuf", [128, 1], F32), "lb0": ("sbuf", [128, 9], F32), "lb": ("sbuf", [128, 9], F32),
     "bl": ("sbuf", [128, 256], BF), "bh": ("sbuf", [128, 256], BF), "bx": ("sbuf", [128, 256], BF),
     "by": ("sbuf", [128, 256], BF), "bs": ("sbuf", [128, 256], BF),
-    "cz": ("sbuf", [128, 1760], BF), "cf": ("sbuf", [128, 384], F32),
-    "z1": ("sbuf", [128, 144], F16), "ones": ("sbuf", [1, 128], BF),
-    "rc1": ("sbuf", [1, 512], BF), "rc2": ("sbuf", [1, 512], BF),
-    "mrow": ("sbuf", [128, 1024], F32), "cio": ("sbuf", [128, 512], F32), "rw": ("sbuf", [128, 64], F32),
-    "mk": ("sbuf", [128, 1536], F32), "oxf": ("sbuf", [128, 1024], F32),
-    "pr8": ("sbuf", [8, 4096], BF), "pt": ("sbuf", [128, 256], BF), "npt": ("sbuf", [128, 512], F32),
-    "hl": ("sbuf", [128, 512], BF), "hp": ("sbuf", [128, 256], BF), "fl": ("sbuf", [128, 528], BF),
-    "ax": ("sbuf", [128, 512], F32), "o16": ("sbuf", [128, 512], F16), "wq": ("sbuf", [128, 512], F32),
-    "ol": ("sbuf", [128, 32], U16), "cm": ("sbuf", [128, 1024], F16), "l1": ("sbuf", [128, 64], U16),
-    "sel": ("sbuf", [128, 1024], BF), "hls": ("sbuf", [128, 1024], BF), "nps": ("sbuf", [128, 1024], F32),
+    "cz": ("sbuf", [128, 2048], BF),
+    "z1": ("sbuf", [128, 144], F16), "zx": ("sbuf", [128, 144], F16), "ones": ("sbuf", [1, 128], BF),
+    "rc1": ("sbuf", [1, 256], BF), "rc2": ("sbuf", [1, 256], BF),
+    "mrow": ("sbuf", [128, 1024], F32), "cio": ("sbuf", [128, 256], BF), "rw": ("sbuf", [128, 64], F32),
+    "mk": ("sbuf", [128, 1280], BF), "pr8": ("sbuf", [8, 4096], BF), "pt": ("sbuf", [128, 256], BF),
+    "nr": ("sbuf", [128, 4096], BF), "ng": ("sbuf", [128, 1024], BF),
+    "hl": ("sbuf", [128, 512], BF), "hr": ("sbuf", [128, 256], F32), "hp": ("sbuf", [128, 256], BF),
+    "p8": ("sbuf", [128, 256], F32), "cd": ("sbuf", [128, 256], F32), "fl": ("sbuf", [128, 256], BF),
+    "f0": ("sbuf", [128, 264], BF), "f1": ("sbuf", [128, 264], BF),
+    "ax": ("sbuf", [128, 256], F32), "o16": ("sbuf", [128, 256], F16), "wq": ("sbuf", [128, 256], F32),
+    "ol": ("sbuf", [128, 16], U16), "cm": ("sbuf", [128, 1024], BF), "l1": ("sbuf", [128, 64], U16),
+    "sel": ("sbuf", [128, 1024], BF), "hls": ("sbuf", [128, 1024], F16), "lo": ("sbuf", [128, 64], U16),
     "l2": ("sbuf", [128, 64], U16), "l3": ("sbuf", [128, 64], U16), "l4": ("sbuf", [128, 64], U16),
     "tb1": ("sbuf", [128, 4112], BF), "tb2": ("sbuf", [128, 4112], BF),
     "r1": ("sbuf", [128, 1024], BF), "r2": ("sbuf", [128, 1024], BF),
     "fl4": ("sbuf", [128, 72], BF), "xn": ("sbuf", [128, 64], F32), "xx": ("sbuf", [128, 64], F32),
     "a4": ("sbuf", [128, 64], F32), "q4": ("sbuf", [128, 64], F32), "o4": ("sbuf", [128, 64], F32),
     "fd": ("sbuf", [128, 1024], F32), "win": ("sbuf", [128, 1408], F32),
-    "landp": ("dram", [128, 256], BF), "pd": ("dram", [128, 256], BF),
+    "landp": ("dram", [128, 256], BF), "pd": ("dram", [128, 256], BF), "nmd": ("dram", [128, 512], BF),
+    "ptd": ("dram", [128, 256], BF),
     "lpt1": ("dram", [128, 256], BF), "lpt2": ("dram", [128, 256], BF), "lhp": ("dram", [128, 256], BF),
     "lhl1": ("dram", [128, 512], BF), "lhl2": ("dram", [128, 512], BF),
 }
@@ -37,7 +40,9 @@ for _b in range(8):
 NE = 138
 SEMAPHORES = ["own_r_s", "landp_s", "lpt1_s", "lpt2_s", "lhl1_s", "lhl2_s", "lhp_s", "ls"] + ["e%d" % _i for _i in range(NE)]
 
-ZS, ZW, ZC, ZP, EP, Z1, OC, ON4, TC, DG, FO, FT, FP = 0, 144, 288, 432, 576, 720, 864, 992, 1120, 1248, 1376, 1504, 1632
+ZS, ZW, ZN, EP, Z1, ZX, ZL, ZU = 0, 144, 288, 432, 576, 720, 864, 1008
+ON4, DG, FO, FT, FP, OC, FN = 1152, 1280, 1408, 1536, 1664, 1792, 1920
+MAGIC = 12582912.0
 
 
 def rank_program(g, core, T, topo):
@@ -76,11 +81,14 @@ def rank_program(g, core, T, topo):
     def landed(q, nm, cnt):
         Q[q].wait_ge(T.sem[nm], cnt)
 
-    def send(dst, out, in_, sem):
+    def send(dst, out, in_, sem, part=None):
         rid, pid = topo.addr(dst)[:2]
+        eng = topo.engines(core, dst)
+        if part is not None:
+            eng = eng[len(eng) // 2 * part:len(eng) // 2 * (part + 1)]
         g.remote_dma(out_ap=out, in_ap=in_, remote_sem=T.sem[sem], local_sem=T.sem.ls, pid=pid, routing_id=rid,
-                     dma_engine_mask=topo.mask(core, dst))
-        ls[0] += len(topo.engines(core, dst))
+                     dma_engine_mask=sum(1 << e for e in eng))
+        ls[0] += len(eng)
 
     def iota(out, pattern, base=0, cm=0):
         return g.iota(out, pattern, base, cm, allow_small_or_imprecise_dtypes=True)
@@ -95,32 +103,44 @@ def rank_program(g, core, T, topo):
     n1, n2 = len(topo.engines(s1, core)), len(topo.engines(s2, core))
     nh = n1 // 2
 
-    t_own = dsig(Y.dma_start(T.own_i[:, :], T.own[:, :]))
     t_pts = dsig(S.dma_start(T.pts_i[:, :], T.pts[:, :]))
+    t_own = dsig(Y.dma_start(T.own_i[:, :], T.own[:, :]))
     t_nxt = dsig(Y.dma_start(T.nxt_i[:, :], T.nxt[:, :]))
 
     k0 = new()
     sig(g.iota(T.pidx[:, :], [[0, 1]], 0, 1), k0)
-    sig(iota(T.lb0[:, :], [[32, 8]]), k0)
-    sig(iota(T.bl[:, :], [[1, 32], [0, 8]]), k0)
-    sig(iota(T.bh[:, :], [[0, 32], [2, 8]]), k0)
+    sig(iota(T.lb0[:, :], [[16, 9]]), k0)
+    sig(iota(T.bl[:, :], [[1, 16], [0, 16]]), k0)
+    sig(iota(T.bh[:, :], [[0, 16], [1, 16]]), k0)
 
     z0 = sig(V.memset(T.zb[:, :], 0.0))
     w("s", z0)
     f_tab = new()
-    for a in range(8192, 16384, 2048):
-        sig(S.activation(T.tab[:, a:a + 2048], T.zb[:, :], F.Copy), f_tab)
+    VT = 7168
+    for a in range(VT, 16384, 2048):
+        b = min(a + 2048, 16384)
+        sig(S.activation(T.tab[:, a:b], T.zb[:, 0:b - a], F.Copy), f_tab)
 
     w("v", k0)
     c1 = new()
     sig(V.tensor_scalar(T.par[:, :], T.pidx[:, :], 1, None, A.bitwise_and), c1)
     sig(V.tensor_scalar(T.p16[:, :], T.pidx[:, :], 15, None, A.bitwise_and), c1)
     w("v", c1)
-    cc = new()
+    cc, cu = new(), new()
     sig(V.tensor_copy(T.colB[:, :], T.par[:, :]), cc)
     sig(V.tensor_scalar(T.colA[:, :], T.par[:, :], 0, None, A.is_equal), cc)
-    sig(V.tensor_scalar(T.colF[:, :], T.p16[:, :], 0, -1.0, A.is_equal, A.mult), cc)
-    sig(V.tensor_scalar(T.colW[:, :], T.par[:, :], -255.0, 256.0, A.mult, A.add), cc)
+    sig(V.tensor_scalar(T.colF[:, :], T.p16[:, :], 0, -1.0, A.is_equal, A.mult), cu)
+    sig(V.tensor_scalar(T.colU[:, :], T.p16[:, :], 256.0, None, A.mult), cu)
+    w("v", t_pts)
+    c_pts = sig(V.tensor_copy(T.ptsb[:, :], T.pts_i[:, :]))
+    w("v", t_own)
+    c_own = sig(V.tensor_copy(T.own_u[:, :], T.own_i[:, :]))
+
+    w("g", c_pts)
+    send(d1, T.landp[:, :], T.ptsb[:, :], "landp_s", 0)
+    w("g", c_own)
+    send(d1, T.own_r[:, :], T.own_u[:, :], "own_r_s", 1)
+
     w("v", cc)
     b1 = new()
     sig(V.tensor_scalar(T.lb[:, :], T.lb0[:, :], T.colB[:, :], None, A.mult), b1)
@@ -128,29 +148,12 @@ def rank_program(g, core, T, topo):
     sig(V.tensor_scalar(T.by[:, :], T.bh[:, :], T.colA[:, :], None, A.mult), b1)
     w("v", b1)
     b2 = sig(V.tensor_tensor(T.bs[:, :], T.bx[:, :], T.by[:, :], A.add))
-    w("v", t_own)
-    c_own = sig(V.tensor_copy(T.own_u[:, :], T.own_i[:, :]))
-    w("v", t_pts)
-    c_pts = sig(V.tensor_copy(T.ptsb[:, :], T.pts_i[:, :]))
-
-    w("g", c_own, c_pts)
-    rid, pid = topo.addr(d1)[:2]
-    eng = topo.engines(core, d1)
-    h = len(eng) // 2
-    g.remote_dma_fused([
-        RemoteDMATransfer(srcs=[T.ptsb[:, :]], dsts=[T.landp[:, :]], dst_ids=[DstId(rid=rid, pnc=pid)],
-                          dma_engine_mask=sum(1 << e for e in eng[:h]), remote_sem=T.sem.landp_s),
-        RemoteDMATransfer(srcs=[T.own_u[:, :]], dsts=[T.own_r[:, :]], dst_ids=[DstId(rid=rid, pnc=pid)],
-                          dma_engine_mask=sum(1 << e for e in eng[h:2 * h]), remote_sem=T.sem.own_r_s)],
-        local_sem=T.sem.ls)
-    ls[0] += 2 * h
-
     w("v", b2)
     dd = new()
     for ch in range(8):
         sig(V.tensor_scalar(T.dat[:, 256 * ch:256 * ch + 256], T.bs[:, :], T.lb[:, ch:ch + 1], None, A.add), dd)
     w("v", dd)
-    dd2 = sig(V.tensor_scalar(T.dat[:, 2048:4096], T.dat[:, 0:2048], T.colA[:, :], None, A.add))
+    dd2 = sig(V.tensor_scalar(T.dat[:, 2048:4096], T.dat[:, 0:2048], T.lb[:, 8:9], None, A.add))
     w("y", c_pts)
     t_pd = dsig(Y.dma_start(T.pd[:, :], T.ptsb[:, :]))
     w("y", t_pd)
@@ -158,13 +161,9 @@ def rank_program(g, core, T, topo):
     w("y", dd, dd2)
     landed("y", "landp_s", nh)
     t_dat = dsig(Y.dma_start(T.dat[2:128:16, :], T.landp[:, :]))
+    f_tabv = sig(V.memset(T.tab[:, 0:VT], 0.0))
     w("v", t_nxt)
     c_nxt = sig(V.tensor_copy(T.nxt_u[:, :], T.nxt_i[:, :]))
-    c_ownf = sig(V.tensor_copy(T.own_f[:, :], T.own_i[:, :]))
-    f_tabv = sig(V.memset(T.tab[:, 0:8192], 0.0))
-    zz = new()
-    sig(V.memset(T.fl[:, 0:8], 0.0), zz)
-    sig(V.memset(T.fl4[:, 0:8], 0.0), zz)
 
     w("v", f_tabv, f_tab, dd, dd2, t_dat)
     landed("v", "own_r_s", nh)
@@ -177,86 +176,73 @@ def rank_program(g, core, T, topo):
             dsig(Y.dma_start(tb[:, a:b], T.zb[:, 0:b - a]), t_tb)
 
     k1 = new()
-    sig(iota(T.cz[:, :], [[0, 1760]]), k1)
-    sig(iota(T.cf[:, :], [[0, 384]]), k1)
+    sig(iota(T.cz[:, :], [[0, 2048]]), k1)
     sig(iota(T.ones[:, :], [[0, 128]], 1), k1)
     w("g", k1)
 
     def view(b, start):
         return T.cz[:, b + start:b + start + 113:16]
 
-    def one(b, start, part, wt):
-        return g.affine_select(view(b, start), view(b, start), [[-16, 8]], A.not_equal, wt, -part, 1)
+    def put(x, part, wt):
+        return g.affine_select(x, x, [[-16, 8]], A.not_equal, wt, -part, 1)
 
     def setw(x, pattern, wt, base, cm):
         return g.affine_select(x, x, pattern, A.is_ge, wt, base, cm)
-    k2 = new()
+    k2, k3, k4, k5, k6 = new(), new(), new(), new(), new()
     ep = T.cz[0:8, EP + 15:EP + 128:16]
     sig(g.affine_select(ep, ep, [[-1, 8]], A.not_equal, 1.0, 0, 1), k2)
-    for hh in range(2):
-        na = T.cf[:, 128 * hh:128 * hh + 128:2]
-        sig(g.affine_select(na, na, [[-16, 8], [-1, 8]], A.not_equal, 1.0, -8 * hh, 1), k2)
-    sig(one(ZS, 14, 0, 1.0), k2)
-    sig(one(ZS, 15, 1, 1.0), k2)
-    sig(one(ZP, 15, 2, 1.0), k2)
-    sig(one(Z1, 15, 0, 1.0), k2)
+    sig(put(view(Z1, 15), 0, 1.0), k2)
     grp = [[16, 8], [0, 16]]
-    vz, ve, vo = view(ZC, 15), T.cf[:, 256:384:16], T.cf[:, 257:384:16]
-    k3, k4 = new(), new()
-    for b, wt in ((OC, 0.5), (ON4, -2048.0), (TC, 0.5), (FO, 1.0), (FT, 1.0)):
+    vx = view(ZX, 15)
+    for b, wt in ((OC, 0.5), (ON4, -2048.0), (FO, 1.0), (FT, 1.0)):
         sig(setw(cz(b), grp, wt, -1, -1), k3)
     sig(g.affine_select(cz(DG), cz(DG), [[-1, 128]], A.not_equal, 2048.0, 0, 1), k3)
-    sig(one(ZW, 15, 0, 256.0), k3)
-    sig(one(FP, 1, 2, 1.0), k3)
-    for x in (vz, ve, vo):
-        sig(setw(x, [[16, 8]], 1.0, -1, -1), k3)
+    sig(setw(vx, [[16, 8]], 1.0, -1, -1), k3)
+    sig(put(view(ZS, 14), 0, 1.0), k3)
+    sig(put(view(ZS, 15), 1, 1.0), k3)
+    sig(put(view(ZN, 15), 0, 256.0), k3)
+    sig(put(view(ZW, 15), 0, 256.0), k3)
+    sig(put(view(FP, 1), 2, 1.0), k3)
+    sig(put(view(FN, 0), 0, 128.0), k3)
+    sig(put(view(FN, 1), 2, 1.0), k3)
     w("g", k3)
     for b in (OC, ON4, FO):
         sig(setw(cz(b), grp, 0.0, 15, -1), k4)
-    sig(setw(cz(TC), [[16, 8], [2, 8], [0, 2]], 0.0, 1, -1), k4)
     sig(setw(cz(FT), [[1, 128]], 0.0, 0, -1), k4)
-    sig(one(ZW, 15, 1, 1.0), k4)
-    sig(one(FP, 1, 3, 1.0), k4)
-    for x in (vz, ve, vo):
-        sig(setw(x, [[16, 8]], 0.0, 15, -1), k4)
-    k5 = new()
-    sig(iota(T.rc1[:, :], [[8, 64], [0, 8]], 1024), k5)
-    sig(iota(T.rc2[:, :], [[0, 64], [1, 8]]), k5)
-    sig(iota(T.cio[:, :], [[1, 512]]), k5)
-    sig(iota(T.mrow[:, :], [[1, 1024]], 2049), k5)
-    sig(iota(T.rw[:, :], [[16, 64]], 264, 1), k5)
+    sig(setw(vx, [[16, 8]], 0.0, 15, -1), k4)
+    sig(put(view(ZN, 15), 1, 1.0), k4)
+    sig(put(view(ZW, 15), 1, 1.0), k4)
+    sig(put(view(FP, 1), 3, 1.0), k4)
+    sig(put(view(FN, 0), 1, 1.0), k4)
+    w("g", k4)
+    sig(put(view(ZN, 15), 2, 16384.0), k5)
+    sig(iota(T.rc1[:, :], [[8, 32], [0, 8]], 1024), k5)
+    sig(iota(T.rc2[:, :], [[0, 32], [1, 8]]), k5)
+    sig(iota(T.cio[:, :], [[1, 256]]), k5)
+    sig(iota(T.mrow[:, :], [[1, 1024]], 2049), k6)
+    sig(iota(T.rw[:, :], [[16, 64]], 264, 1), k6)
 
-    fo, fm = new(), new()
-    sig(S.activation(T.oxf[:, 0:1024], T.zb[:, 0:1024], F.Copy), fo)
-    w("s", fo, c_ownf, cc)
-    ox = new()
-    sig(S.activation(T.oxf[:, 0:512:2], T.own_f[:, :], F.Copy), ox)
-    sig(S.activation(T.oxf[:, 513:1024:2], T.own_f[:, :], F.Copy), ox)
+    fm = new()
     sig(S.activation(T.mk[:, 0:1024], T.zb[:, 0:1024], F.Copy), fm)
+    w("s", cu)
     sig(S.activation(T.win[:, 0:264], T.zb[:, 0:264], F.Identity, bias=T.colF[:, :]), fm)
     w("p", t_pr8, k2)
     for kk in range(16):
-        k, hh = kk // 2, kk % 2
-        m = mm(ps[2][:, 0:256], cz(EP + 15 - kk, 128, 8), T.pr8[:, hh * 2048 + k:hh * 2048 + 2048:8], kk == 0, kk == 15)
+        m = mm(ps[2][:, 0:256], cz(EP + 15 - kk, 128, 8), T.pr8[:, kk:4096:16], kk == 0, kk == 15)
     m_pt = sig(m)
-    w("p", ox)
-    for hh in range(2):
-        mm(ps[3][:, :], T.cf[:, 128 * hh:128 * hh + 128], T.oxf[:, 512 * hh:512 * hh + 512], hh == 0, False)
-    for k in range(8):
-        m = mm(ps[3][:, :], cz(EP + 14 - 2 * k, 128, 8), T.pr8[:, k:4096:8], False, k == 7)
-    m_np = sig(m)
     w("s", m_pt)
     c_pt = sig(S.activation(T.pt[:, :], ps[2][:, 0:256], F.Copy))
-    w("s", m_np)
-    c_np = sig(S.activation(T.npt[:, :], ps[3][:, :], F.Copy))
     w("s", k4)
     ksc = new()
-    sig(S.activation(vz, vz, F.Copy, scale=T.colW[:, :]), ksc)
-    sig(S.activation(ve, ve, F.Copy, scale=T.colA[:, :]), ksc)
-    sig(S.activation(vo, vo, F.Copy, scale=T.colB[:, :]), ksc)
+    sig(S.activation(view(ZL, 15), vx, F.Copy, scale=4096.0), ksc)
+    sig(S.activation(view(ZU, 15), vx, F.Copy, scale=T.colU[:, :]), ksc)
+    fnr = new()
+    sig(S.activation(T.nr[:, 0:2048], T.zb[:, :], F.Copy), fnr)
     w("g", c_pt)
     send(d1, T.lpt1[:, :], T.pt[:, :], "lpt1_s")
     send(d2, T.lpt2[:, :], T.pt[:, :], "lpt2_s")
+    w("y", c_pt)
+    t_ptd = dsig(Y.dma_start(T.ptd[:, :], T.pt[:, :]))
     w("y", t_tb)
     tab1, tab2 = new(), new()
     landed("y", "lpt1_s", n1)
@@ -271,97 +257,134 @@ def rank_program(g, core, T, topo):
         for j in (i, i + 2):
             o, src = T.gat[:, 1024 * j:1024 * j + 1024], T.tab[:, :].indirect(T.nxt_u[:, 64 * j:64 * j + 64])
             gt[j] = sig(V.tensor_copy(o, src) if j < 2 else S.activation(o, src, F.Copy))
-    m_hl = [new(), new()]
-    for j in (0, 2, 1, 3):
+    m_cd, m_hl = new(), [new(), new()]
+
+    def fold_code(j):
+        for kk in range(16):
+            m = mm(ps[6][:, 64 * j:64 * j + 64], cz(ZN + 15 - kk), T.gat[:, 1024 * j + kk:1024 * j + 1024:16],
+                   kk == 0, kk == 15)
+        sig(m, m_cd)
+
+    def fold_pair(j):
+        for hh in range(2):
+            for k in range(8):
+                m = mm(ps[hh][:, 64 * j:64 * j + 64], cz(ZS + 14 - 2 * k),
+                       T.gat[:, 1024 * j + 8 * hh + k:1024 * j + 1024:16], k == 0, k == 7)
+            sig(m, m_hl[hh])
+    w("p", k3, k4, k5)
+    for j in (0, 2):
         w("p", gt[j])
-        b, c0 = j // 2, 128 * (j % 2)
-        for k in range(8):
-            m = mm(ps[b][:, c0:c0 + 128], cz(ZS + 14 - 2 * k), T.gat[:, 1024 * j + k:1024 * j + 1024:8], k == 0, k == 7)
-        sig(m, m_hl[b])
+        fold_pair(j)
+    fold_code(0)
+    for j in (1, 3):
+        w("p", gt[j])
+        fold_pair(j)
+
+    zz, nm0, nm1 = new(), new(), new()
+    sig(V.memset(T.f0[:, 0:8], 0.0), zz)
+    sig(V.memset(T.f1[:, 0:8], 0.0), zz)
+    sig(V.tensor_scalar(T.onh[:, :], T.own_i[:, :], 7, None, A.arith_shift_right), nm0)
+    sig(V.tensor_scalar(T.onl[:, :], T.own_i[:, :], 127, None, A.bitwise_and), nm0)
     w("v", m_hl[0])
-    hla = sig(V.tensor_copy(T.hl[:, 0:256], ps[0][:, 0:256]))
+    f0 = sig(V.tensor_scalar(T.f0[:, 8:264], ps[0][:, 0:256], 0.0, None, A.is_gt))
     w("s", m_hl[1])
+    f1 = sig(S.activation(T.f1[:, 8:264], ps[1][:, 0:256], F.Sign))
     hlb = sig(S.activation(T.hl[:, 256:512], ps[1][:, 0:256], F.Copy))
+    hla = sig(V.tensor_copy(T.hl[:, 0:256], ps[0][:, 0:256]))
+    w("p", f0, f1, zz, c_pt, k1)
+    mm(ps[2][:, 0:256], cz(OC), T.f0[:, 7:263], True, False)
+    m_c = sig(mm(ps[2][:, 0:256], cz(OC), T.f1[:, 7:263], False, True))
+    mm(ps[3][:, 0:256], cz(ON4), T.f0[:, 8:264], True, False)
+    mm(ps[3][:, 0:256], cz(ON4), T.f1[:, 8:264], False, False)
+    mm(ps[3][:, 0:256], T.ones[:, :], T.rc1[:, :], False, False)
+    m_x = sig(mm(ps[3][:, 0:256], T.ones[:, :], T.rc2[:, :], False, True))
+    fold_code(2)
     w("g", hla, hlb)
     send(d1, T.lhl1[:, :], T.hl[:, :], "lhl1_s")
     send(d2, T.lhl2[:, :], T.hl[:, :], "lhl2_s")
-    landed("y", "lhl1_s", n1)
-    dsig(Y.dma_start(T.tb1[0:128:16, 16:4112], T.lhl1[0:128:2, :]), tab1)
-    dsig(Y.dma_start(T.tb1[1:128:16, 16:4112], T.lhl1[1:128:2, :]), tab1)
-    landed("y", "lhl2_s", n2)
-    dsig(Y.dma_start(T.tb2[0:128:16, 16:4112], T.lhl2[0:128:2, :]), tab2)
-    dsig(Y.dma_start(T.tb2[1:128:16, 16:4112], T.lhl2[1:128:2, :]), tab2)
-
-    w("v", hla, hlb, zz)
-    fl = sig(V.tensor_scalar(T.fl[:, 8:520], T.hl[:, :], 0.0, None, A.is_gt))
+    w("v", m_c, z0)
+    ta = sig(V.tensor_tensor_scan(T.ax[:, :], ps[2][:, 0:256], T.zb[:, 0:256], 0.0, A.add, A.add))
     w("v", k2)
     z1h = sig(V.tensor_copy(T.z1[:, :], cz(Z1, 144)))
-    flx, fls = T.fl[:, 8:520], T.fl[:, 7:519]
-    w("p", fl, zz, k3, k4, c_pt)
-    m_c = sig(mm(ps[2][:, :], cz(OC), fls, True, True))
-    w("p", k1, k5, c_np)
-    mm(ps[3][:, :], cz(ON4), flx, True, False)
-    mm(ps[3][:, :], T.ones[:, :], T.rc1[:, :], False, False)
-    m_x = sig(mm(ps[3][:, :], T.ones[:, :], T.rc2[:, :], False, True))
-
-    def hp(lo, hi):
-        m = None
-        for kk in range(lo, hi):
-            k, hh = kk // 2, kk % 2
-            m = mm(ps[0][:, 0:256], cz(ZP + 15 - kk), T.gat[:, hh * 2048 + k:hh * 2048 + 2048:8], kk == 0, kk == 15)
-        return m
-    w("p", hla)
-    hp(0, 4)
-    w("v", m_c, z0)
-    ta = sig(V.tensor_tensor_scan(T.ax[:, :], ps[2][:, :], T.zb[:, 0:512], 0.0, A.add, A.add))
     w("v", ta, m_x)
-    to = sig(V.tensor_tensor(T.o16[:, :], T.ax[:, :], ps[3][:, :], A.max))
-    w("p", to, z1h)
+    to = sig(V.tensor_tensor(T.o16[:, :], T.ax[:, :], ps[3][:, 0:256], A.max))
+    w("p", z1h, to)
     for k in range(16):
-        m = mm(ps[5][:, 0:32], T.z1[:, 15 - k:143 - k], T.o16[:, k:512:16], k == 0, k == 15)
+        m = mm(ps[5][:, 0:16], T.z1[:, 15 - k:143 - k], T.o16[:, k:256:16], k == 0, k == 15)
     m_o = sig(m)
-    mm(ps[4][:, :], cz(TC), flx, True, False)
-    m_p = sig(mm(ps[4][:, :], cz(DG), flx, False, True))
-    m_hp = sig(hp(4, 16))
+    fold_code(1)
+    fold_code(3)
+    w("v", nm0)
+    sig(V.tensor_copy(T.nmb[:, 0:256], T.onh[:, :]), nm1)
+    sig(V.tensor_copy(T.nmb[:, 256:512], T.onl[:, :]), nm1)
+    sig(S.activation(T.nr[:, 2048:4096], T.zb[:, :], F.Copy), fnr)
     w("v", m_o)
-    tol = sig(V.tensor_copy(T.ol[:, :], ps[5][:, 0:32]))
+    tol = sig(V.tensor_copy(T.ol[:, :], ps[5][:, 0:16]))
     w("v", tol, fm, k5)
     tmk = sig(V.tensor_copy(T.mk[:, :].indirect(T.ol[:, :]), T.cio[:, :]))
-    w("v", m_p)
-    twq = sig(V.tensor_tensor(T.wq[:, :], T.ax[:, :], ps[4][:, :], A.add))
     w("v", tmk)
     tcm = sig(V.tensor_tensor_scan(T.cm[:, :], T.mk[:, 0:1024], T.zb[:, 0:1024], 0.0, A.max, A.max))
-    w("s", m_hp)
-    c_hp = sig(S.activation(T.hp[:, :], ps[0][:, 0:256], F.Copy))
-    w("g", c_hp)
-    send(d2, T.lhp[:, :], T.hp[:, :], "lhp_s")
-    landed("y", "lhp_s", n2)
-    dsig(Y.dma_start(T.tb2[3:128:16, 16:4112], T.lhp[:, :]), tab2)
     w("p", tcm)
     for k in range(16):
-        m = mm(ps[5][:, 64:128], T.z1[:, 15 - k:143 - k], T.cm[:, k:1024:16], k == 0, k == 15)
+        m = mm(ps[5][:, 64:128], cz(Z1 + 15 - k), T.cm[:, k:1024:16], k == 0, k == 15)
     m_l1 = sig(m)
+    w("s", m_cd)
+    x1 = sig(S.activation(T.hr[:, :], ps[6][:, 0:256], F.Identity, bias=MAGIC, scale=1.0 / 16384))
+    w("s", x1)
+    c_hp = sig(S.activation(T.hp[:, :], T.hr[:, :], F.Identity, bias=-MAGIC))
+    w("s", c_hp)
+    c_p8 = sig(S.activation(T.p8[:, :], T.hp[:, :], F.Identity, bias=2304.0, scale=16384.0))
+    w("g", c_hp)
+    send(d2, T.lhp[:, :], T.hp[:, :], "lhp_s")
+    w("v", x1)
+    fl = sig(V.tensor_scalar(T.fl[:, :], ps[6][:, 0:256], 0.0, None, A.is_gt))
+    sig(V.memset(T.fl4[:, 0:8], 0.0), zz)
+    w("p", fl)
+    mm(ps[4][:, 0:256], cz(FT), T.fl[:, :], True, False)
+    m_p = sig(mm(ps[4][:, 0:256], cz(DG), T.fl[:, :], False, True))
+    for k in range(16):
+        mm(ps[7][:, 0:64], cz(Z1 + 15 - k), T.cm[:, k:1024:16], k == 0, False)
+    w("y", nm1)
+    t_nmd = dsig(Y.dma_start(T.nmd[:, :], T.nmb[:, :]))
+    t_nr = new()
+    w("s", fnr, t_nmd, t_ptd)
+    dsig(S.dma_start(T.nr[0:128:16, :], T.nmd[:, 0:256]), t_nr)
+    dsig(S.dma_start(T.nr[1:128:16, :], T.nmd[:, 256:512]), t_nr)
+    dsig(S.dma_start(T.nr[2:128:16, :], T.ptd[:, :]), t_nr)
+    for tb, ld, sm, cnt, tk in ((T.tb1, T.lhl1, "lhl1_s", n1, tab1), (T.tb2, T.lhl2, "lhl2_s", n2, tab2)):
+        landed("y", sm, cnt)
+        for s_ in range(2):
+            for hh in range(2):
+                dsig(Y.dma_start(tb[s_:128:16, 16 + 2048 * hh:2064 + 2048 * hh], ld[s_:128:2, 256 * hh:256 * hh + 256]), tk)
+    landed("y", "lhp_s", n2)
+    dsig(Y.dma_start(T.tb2[3:128:16, 16:4112], T.lhp[:, :]), tab2)
+
     w("v", m_l1)
     tl1 = sig(V.tensor_copy(T.l1[:, :], ps[5][:, 64:128]))
-    w("v", tl1, twq)
+    w("v", m_p)
+    twq = sig(V.tensor_tensor(T.wq[:, :], T.ax[:, :], ps[4][:, 0:256], A.add))
+    w("v", tl1, twq, k6)
     tse = sig(V.tensor_tensor(T.sel[:, :], T.wq[:, :].indirect(T.l1[:, :]), T.mrow[:, :], A.is_equal))
-    w("v", tse)
-    ths = sig(V.tensor_tensor(T.hls[:, :], T.hl[:, :].indirect(T.l1[:, :]), T.sel[:, :], A.mult))
-    w("p", ths, ksc)
+    w("v", c_p8)
+    tcd = sig(V.tensor_tensor(T.cd[:, :], ps[6][:, 0:256], T.p8[:, :], A.subtract))
+    w("v", k4)
+    zxh = sig(V.tensor_copy(T.zx[:, :], cz(ZX, 144)))
+    w("v", tse, tcd)
+    ths = sig(V.tensor_tensor(T.hls[:, :], T.cd[:, :].indirect(T.l1[:, :]), T.sel[:, :], A.mult))
+    w("p", tse, ksc)
     for k in range(16):
-        m = mm(ps[5][:, 128:192], cz(ZC + 15 - k), T.hls[:, k:1024:16], k == 0, k == 15)
+        mm(ps[5][:, 128:192], cz(ZL + 15 - k), T.sel[:, k:1024:16], k == 0, False)
+    for k in range(16):
+        m = mm(ps[7][:, 0:64], cz(ZU + 15 - k), T.sel[:, k:1024:16], False, k == 15)
+    m_lo = sig(m)
+    w("p", ths, zxh)
+    for k in range(16):
+        m = mm(ps[5][:, 128:192], T.zx[:, 15 - k:143 - k], T.hls[:, k:1024:16], False, k == 15)
     m_l2 = sig(m)
-    w("v", c_np)
-    tnp = []
-    for hh in range(2):
-        sl = slice(512 * hh, 512 * hh + 512)
-        tnp.append(sig(V.tensor_tensor(T.nps[:, sl], T.npt[:, :].indirect(T.l1[:, 32 * hh:32 * hh + 32]), T.sel[:, sl], A.mult)))
-        if hh == 0:
-            w("v", m_l2)
-            tl2 = sig(V.tensor_scalar(T.l2[:, :], ps[5][:, 128:192], -241.0, None, A.add))
-    for hh in range(2):
-        w("p", tnp[hh])
-        mm(ps[6 + hh][:, :], T.cf[:, 256:384], T.nps[:, 512 * hh:512 * hh + 512], True, False)
+    w("v", m_lo)
+    tlo = sig(V.tensor_copy(T.lo[:, :], ps[7][:, 0:64]))
+    w("v", m_l2)
+    tl2 = sig(V.tensor_scalar(T.l2[:, :], ps[5][:, 128:192], -2033.0, None, A.add))
 
     def pick(tb, lst, out, toks):
         ts = []
@@ -371,27 +394,32 @@ def rank_program(g, core, T, topo):
             ts.append(sig(V.tensor_copy(out[:, sl], src) if q == "v" else S.activation(out[:, sl], src, F.Copy)))
         return ts
     tr1 = pick(T.tb1, T.l2, T.r1, [tl2, tab1])
-    w("p", hlb, *tr1)
+    tng = pick(T.nr, T.lo, T.ng, [tlo, t_nr])
+    w("p", hlb, tcd, tlo, *tr1)
     for k in range(16):
         m = mm(ps[1][:, 0:64], cz(ZW + 15 - k), T.r1[:, k:1024:16], k == 0, k == 15)
     m_l3 = sig(m)
     for hh in range(2):
-        mm(ps[6 + hh][:, :], cz(FP), T.r1[:, 512 * hh:512 * hh + 512], False, False)
+        mm(ps[6 + hh][:, :], cz(FP), T.r1[:, 512 * hh:512 * hh + 512], True, False)
     w("v", m_l3)
     tl3 = sig(V.tensor_scalar(T.l3[:, :], ps[1][:, 0:64], -241.0, None, A.add))
     tr2 = pick(T.tb2, T.l3, T.r2, [tl3, tab2])
+    for hh in range(2):
+        w("p", tng[hh])
+        mm(ps[6 + hh][:, :], cz(FN), T.ng[:, 512 * hh:512 * hh + 512], False, False)
     w("p", *tr2)
     for k in range(16):
         m = mm(ps[1][:, 64:128], cz(ZW + 15 - k), T.r2[:, k:1024:16], k == 0, k == 15)
     m_l4 = sig(m)
-    m_fd = [sig(mm(ps[6 + hh][:, :], cz(FP), T.r2[:, 512 * hh:512 * hh + 512], False, True)) for hh in range(2)]
+    m_fd = [sig(mm(ps[6][:, :], cz(FP), T.r2[:, 0:512], False, True))]
 
     w("v", m_l4)
     f4 = sig(V.tensor_scalar(T.fl4[:, 8:72], ps[1][:, 64:128], 0.0, None, A.is_gt))
     x1 = sig(V.tensor_scalar(T.xn[:, :], ps[1][:, 64:128], 0.0, -4096.0, A.is_gt, A.mult))
-    w("p", f4)
+    w("p", f4, zz)
     m_a = sig(mm(ps[2][:, 0:64], cz(FO), T.fl4[:, 7:71], True, True))
     m_q = sig(mm(ps[3][:, 0:64], cz(FT), T.fl4[:, 8:72], True, True))
+    m_fd.append(sig(mm(ps[7][:, :], cz(FP), T.r2[:, 512:1024], False, True)))
     w("v", x1)
     x2 = sig(V.tensor_tensor(T.xx[:, :], T.xn[:, :], T.rw[:, :], A.add))
     tfd = []

@@ -5,11 +5,11 @@ SCRATCH = {
     "own_i": ("sbuf", [128, 256], I32), "nxt_i": ("sbuf", [128, 256], I32), "pts_i": ("sbuf", [128, 256], I32),
     "own_u": ("sbuf", [128, 256], U16), "nxt_u": ("sbuf", [128, 256], U16), "own_r": ("sbuf", [128, 256], U16),
     "onh": ("sbuf", [128, 256], I32), "onl": ("sbuf", [128, 256], I32), "nmb": ("sbuf", [128, 512], BF),
-    "ptsb": ("sbuf", [128, 256], BF), "zb": ("sbuf", [128, 2048], BF),
+    "ptsb": ("sbuf", [128, 256], BF), "zb": ("sbuf", [128, 1024], BF),
     "tab": ("sbuf", [128, 16384], BF), "dat": ("sbuf", [128, 4096], BF), "gat": ("sbuf", [128, 4096], BF),
     "pidx": ("sbuf", [128, 1], I32), "par": ("sbuf", [128, 1], I32), "p16": ("sbuf", [128, 1], I32),
     "colA": ("sbuf", [128, 1], F32), "colB": ("sbuf", [128, 1], F32), "colF": ("sbuf", [128, 1], F32),
-    "colU": ("sbuf", [128, 1], F32), "lb0": ("sbuf", [128, 9], F32), "lb": ("sbuf", [128, 9], F32),
+    "colU": ("sbuf", [128, 1], F32), "lb0": ("sbuf", [128, 16], F32), "lb": ("sbuf", [128, 16], F32),
     "bl": ("sbuf", [128, 256], BF), "bh": ("sbuf", [128, 256], BF), "bx": ("sbuf", [128, 256], BF),
     "by": ("sbuf", [128, 256], BF), "bs": ("sbuf", [128, 256], BF),
     "cz": ("sbuf", [128, 2048], BF),
@@ -17,32 +17,33 @@ SCRATCH = {
     "rc1": ("sbuf", [1, 256], BF), "rc2": ("sbuf", [1, 256], BF),
     "mrow": ("sbuf", [128, 1024], F32), "cio": ("sbuf", [128, 256], BF), "rw": ("sbuf", [128, 64], F32),
     "mk": ("sbuf", [128, 1280], BF), "pr8": ("sbuf", [8, 4096], BF), "pt": ("sbuf", [128, 256], BF),
-    "nr": ("sbuf", [128, 4096], BF), "ng": ("sbuf", [128, 1024], BF),
-    "hl": ("sbuf", [128, 512], BF), "hr": ("sbuf", [128, 256], F32), "hp": ("sbuf", [128, 256], BF),
-    "p8": ("sbuf", [128, 256], F32), "cd": ("sbuf", [128, 256], F32), "fl": ("sbuf", [128, 256], BF),
-    "f0": ("sbuf", [128, 264], BF), "f1": ("sbuf", [128, 264], BF),
+    "ng": ("sbuf", [128, 1024], BF), "hl": ("sbuf", [128, 512], BF), "hr": ("sbuf", [128, 256], F32),
+    "p5": ("sbuf", [128, 256], F32), "p8": ("sbuf", [128, 256], F32), "cd": ("sbuf", [128, 256], F32),
+    "fl": ("sbuf", [128, 264], BF),
     "ax": ("sbuf", [128, 256], F32), "o16": ("sbuf", [128, 256], F16), "wq": ("sbuf", [128, 256], F32),
     "ol": ("sbuf", [128, 16], U16), "cm": ("sbuf", [128, 1024], BF), "l1": ("sbuf", [128, 64], U16),
-    "sel": ("sbuf", [128, 1024], BF), "hls": ("sbuf", [128, 1024], F16), "lo": ("sbuf", [128, 64], U16),
-    "l2": ("sbuf", [128, 64], U16), "l3": ("sbuf", [128, 64], U16), "l4": ("sbuf", [128, 64], U16),
+    "sel": ("sbuf", [128, 1024], BF), "hls": ("sbuf", [128, 1024], F16),
+    "ll": ("sbuf", [128, 128], U16), "l3": ("sbuf", [128, 64], U16), "l4": ("sbuf", [128, 64], U16),
+    "l5": ("sbuf", [128, 64], U16),
     "tb1": ("sbuf", [128, 4112], BF), "tb2": ("sbuf", [128, 4112], BF),
-    "r1": ("sbuf", [128, 1024], BF), "r2": ("sbuf", [128, 1024], BF),
+    "r1": ("sbuf", [128, 1024], BF), "r2": ("sbuf", [128, 1024], BF), "r3": ("sbuf", [128, 1024], BF),
     "fl4": ("sbuf", [128, 72], BF), "xn": ("sbuf", [128, 64], F32), "xx": ("sbuf", [128, 64], F32),
     "a4": ("sbuf", [128, 64], F32), "q4": ("sbuf", [128, 64], F32), "o4": ("sbuf", [128, 64], F32),
     "fd": ("sbuf", [128, 1024], F32), "win": ("sbuf", [128, 1408], F32),
-    "landp": ("dram", [128, 256], BF), "pd": ("dram", [128, 256], BF), "nmd": ("dram", [128, 512], BF),
-    "ptd": ("dram", [128, 256], BF),
-    "lpt1": ("dram", [128, 256], BF), "lpt2": ("dram", [128, 256], BF), "lhp": ("dram", [128, 256], BF),
+    "lpt1": ("dram", [128, 256], BF), "lpt2": ("dram", [128, 256], BF), "lpt3": ("dram", [128, 256], BF),
     "lhl1": ("dram", [128, 512], BF), "lhl2": ("dram", [128, 512], BF),
 }
 for _b in range(8):
     SCRATCH["ps%d" % _b] = ("psum", [128, 512], F32)
 NE = 138
-SEMAPHORES = ["own_r_s", "landp_s", "lpt1_s", "lpt2_s", "lhl1_s", "lhl2_s", "lhp_s", "ls"] + ["e%d" % _i for _i in range(NE)]
+SEMAPHORES = ["own_r_s", "lpt1_s", "lpt2_s", "lpt3_s", "lhl1_s", "lhl2_s", "ls"] + ["e%d" % _i for _i in range(NE)]
 
-ZS, ZW, ZN, EP, Z1, ZX, ZL, ZU = 0, 144, 288, 432, 576, 720, 864, 1008
-ON4, DG, FO, FT, FP, OC, FN = 1152, 1280, 1408, 1536, 1664, 1792, 1920
+ZW, ZN, EP, Z1, ZX, ZL, ZU = 144, 288, 432, 576, 720, 864, 1008
+ON4, DG, FO, FT, FP, FN, FQ = 1152, 1280, 1408, 1536, 1664, 1792, 1920
 MAGIC = 12582912.0
+TG, TD, TS = 768, 2048, 5632
+AE = 1536
+NG = 28
 
 
 def rank_program(g, core, T, topo):
@@ -50,8 +51,8 @@ def rank_program(g, core, T, topo):
     if r is None:
         return
     n = len(T.cores)
-    d1, d2 = T.cores[(r - 1) % n], T.cores[(r - 2) % n]
-    s1, s2 = T.cores[(r + 1) % n], T.cores[(r + 2) % n]
+    d1, d2, d3 = (T.cores[(r - k) % n] for k in (1, 2, 3))
+    s1, s2, s3 = (T.cores[(r + k) % n] for k in (1, 2, 3))
     V, S, P, Y = g.vector, g.scalar, g.tensor, g.sync
     Q = {"g": g, "v": V, "s": S, "p": P, "y": Y}
     ctr, seen, waited, made, ls = [0], {}, {}, [], [0]
@@ -78,14 +79,12 @@ def rank_program(g, core, T, topo):
                 seen[(q, t[0])] = t[1]
                 waited[t[0]] = t[1]
 
-    def landed(q, nm, cnt):
-        Q[q].wait_ge(T.sem[nm], cnt)
+    def landed(q, nm, src):
+        Q[q].wait_ge(T.sem[nm], len(topo.engines(src, core)))
 
-    def send(dst, out, in_, sem, part=None):
+    def send(dst, out, in_, sem):
         rid, pid = topo.addr(dst)[:2]
         eng = topo.engines(core, dst)
-        if part is not None:
-            eng = eng[len(eng) // 2 * part:len(eng) // 2 * (part + 1)]
         g.remote_dma(out_ap=out, in_ap=in_, remote_sem=T.sem[sem], local_sem=T.sem.ls, pid=pid, routing_id=rid,
                      dma_engine_mask=sum(1 << e for e in eng))
         ls[0] += len(eng)
@@ -100,85 +99,88 @@ def rank_program(g, core, T, topo):
         return P.matmul(out, lhsT, rhs, first, last)
 
     ps = [T["ps%d" % b] for b in range(8)]
-    n1, n2 = len(topo.engines(s1, core)), len(topo.engines(s2, core))
-    nh = n1 // 2
 
-    t_pts = dsig(S.dma_start(T.pts_i[:, :], T.pts[:, :]))
     t_own = dsig(Y.dma_start(T.own_i[:, :], T.own[:, :]))
-    t_nxt = dsig(Y.dma_start(T.nxt_i[:, :], T.nxt[:, :]))
+    t_nxt = dsig(S.dma_start(T.nxt_i[:, :], T.nxt[:, :]))
+    t_pts = dsig(Y.dma_start(T.pts_i[:, :], T.pts[:, :]))
 
-    k0 = new()
+    k0, k1, k5 = new(), new(), new()
     sig(g.iota(T.pidx[:, :], [[0, 1]], 0, 1), k0)
-    sig(iota(T.lb0[:, :], [[16, 9]]), k0)
-    sig(iota(T.bl[:, :], [[1, 16], [0, 16]]), k0)
-    sig(iota(T.bh[:, :], [[0, 16], [1, 16]]), k0)
+    sig(iota(T.lb0[:, :], [[16, 16]]), k0)
+    sig(iota(T.bl[:, :], [[1, 16], [0, 16]]), k1)
+    sig(iota(T.bh[:, :], [[0, 16], [1, 16]]), k1)
 
     z0 = sig(V.memset(T.zb[:, :], 0.0))
     w("s", z0)
-    f_tab = new()
-    VT = 7168
-    for a in range(VT, 16384, 2048):
-        b = min(a + 2048, 16384)
+    f_tab, f_tabv, t_tab, t_cz = new(), new(), new(), new()
+    for a in range(TG + TD, TG + TD + TS, 1024):
+        b = min(a + 1024, TG + TD + TS)
         sig(S.activation(T.tab[:, a:b], T.zb[:, 0:b - a], F.Copy), f_tab)
+    w("y", z0)
+    for a in range(TG, TG + TD, 1024):
+        dsig(Y.dma_start(T.tab[:, a:a + 1024], T.zb[:, :]), t_tab)
+    for a in (0, 1024):
+        dsig(Y.dma_start(T.cz[:, a:a + 1024], T.zb[:, :]), t_cz)
+    V0 = TG + TD + TS
+    VE = V0 + 2048
+    sig(V.memset(T.tab[:, V0:VE], 0.0), f_tabv)
 
     w("v", k0)
-    c1 = new()
+    c1, cc = new(), new()
     sig(V.tensor_scalar(T.par[:, :], T.pidx[:, :], 1, None, A.bitwise_and), c1)
     sig(V.tensor_scalar(T.p16[:, :], T.pidx[:, :], 15, None, A.bitwise_and), c1)
     w("v", c1)
-    cc, cu = new(), new()
     sig(V.tensor_copy(T.colB[:, :], T.par[:, :]), cc)
     sig(V.tensor_scalar(T.colA[:, :], T.par[:, :], 0, None, A.is_equal), cc)
-    sig(V.tensor_scalar(T.colF[:, :], T.p16[:, :], 0, -1.0, A.is_equal, A.mult), cu)
-    sig(V.tensor_scalar(T.colU[:, :], T.p16[:, :], 256.0, None, A.mult), cu)
-    w("v", t_pts)
-    c_pts = sig(V.tensor_copy(T.ptsb[:, :], T.pts_i[:, :]))
-    w("v", t_own)
-    c_own = sig(V.tensor_copy(T.own_u[:, :], T.own_i[:, :]))
-
-    w("g", c_pts)
-    send(d1, T.landp[:, :], T.ptsb[:, :], "landp_s", 0)
-    w("g", c_own)
-    send(d1, T.own_r[:, :], T.own_u[:, :], "own_r_s", 1)
-
-    w("v", cc)
+    w("v", cc, k1)
     b1 = new()
     sig(V.tensor_scalar(T.lb[:, :], T.lb0[:, :], T.colB[:, :], None, A.mult), b1)
     sig(V.tensor_scalar(T.bx[:, :], T.bl[:, :], T.colB[:, :], 1.0, A.mult, A.add), b1)
     sig(V.tensor_scalar(T.by[:, :], T.bh[:, :], T.colA[:, :], None, A.mult), b1)
+    w("v", t_own)
+    c_own = sig(V.tensor_copy(T.own_u[:, :], T.own_i[:, :]))
     w("v", b1)
     b2 = sig(V.tensor_tensor(T.bs[:, :], T.bx[:, :], T.by[:, :], A.add))
     w("v", b2)
-    dd = new()
-    for ch in range(8):
-        sig(V.tensor_scalar(T.dat[:, 256 * ch:256 * ch + 256], T.bs[:, :], T.lb[:, ch:ch + 1], None, A.add), dd)
-    w("v", dd)
-    dd2 = sig(V.tensor_scalar(T.dat[:, 2048:4096], T.dat[:, 0:2048], T.lb[:, 8:9], None, A.add))
-    w("y", c_pts)
-    t_pd = dsig(Y.dma_start(T.pd[:, :], T.ptsb[:, :]))
-    w("y", t_pd)
-    t_pr8 = dsig(Y.dma_start(T.pr8[:, :], T.pd[:, :]))
-    w("y", dd, dd2)
-    landed("y", "landp_s", nh)
-    t_dat = dsig(Y.dma_start(T.dat[2:128:16, :], T.landp[:, :]))
-    f_tabv = sig(V.memset(T.tab[:, 0:VT], 0.0))
+    da, db = new(), new()
+    for ch in range(AE // 256):
+        sig(V.tensor_scalar(T.dat[:, 256 * ch:256 * ch + 256], T.bs[:, :], T.lb[:, ch:ch + 1], None, A.add), da)
+    w("v", t_pts)
+    c_pts = sig(V.tensor_copy(T.ptsb[:, :], T.pts_i[:, :]))
     w("v", t_nxt)
     c_nxt = sig(V.tensor_copy(T.nxt_u[:, :], T.nxt_i[:, :]))
+    sig(V.memset(T.tab[:, VE:16384], 0.0), f_tabv)
+    cu = new()
+    sig(V.tensor_scalar(T.colF[:, :], T.p16[:, :], 0, -1.0, A.is_equal, A.mult), cu)
+    sig(V.tensor_scalar(T.colU[:, :], T.p16[:, :], 256.0, None, A.mult), cu)
+    w("s", b1, b2)
+    for ch in range(AE // 256, 16):
+        sig(S.activation(T.dat[:, 256 * ch:256 * ch + 256], T.bs[:, :], F.Identity, bias=T.lb[:, ch:ch + 1]), db)
 
-    w("v", f_tabv, f_tab, dd, dd2, t_dat)
-    landed("v", "own_r_s", nh)
-    t_sc = sig(V.tensor_copy(T.tab[:, :].indirect(T.own_r[:, :]), T.dat[:, :]))
+    w("g", c_own)
+    send(d1, T.own_r[:, :], T.own_u[:, :], "own_r_s")
+    sig(iota(T.ones[:, :], [[0, 128]], 1), k5)
+    sig(iota(T.rc1[:, :], [[8, 32], [0, 8]], 1024), k5)
+    sig(iota(T.rc2[:, :], [[0, 32], [1, 8]]), k5)
+    sig(iota(T.cio[:, :], [[1, 256]]), k5)
+    zz = new()
+    sig(iota(T.tab[:, 0:TG], [[0, TG]]), f_tab)
+    sig(iota(T.fl[:, 0:8], [[0, 8]]), zz)
+    sig(iota(T.fl4[:, 0:8], [[0, 8]]), zz)
 
-    w("y", z0)
+    w("v", f_tab, f_tabv, t_tab, da)
+    landed("v", "own_r_s", s1)
+    t_s0 = sig(V.tensor_copy(T.tab[:, :].indirect(T.own_r[:, 0:AE // 16]), T.dat[:, 0:AE]))
+    w("v", db, t_s0)
+    t_sc = sig(V.tensor_copy(T.tab[:, :].indirect(T.own_r[:, AE // 16:256]), T.dat[:, AE:4096]))
+
+    w("y", c_pts)
+    t_pr8 = dsig(Y.dma_start(T.pr8[:, :], T.ptsb[:, :]))
     t_tb = new()
     for tb in (T.tb1, T.tb2):
-        for a, b in ((0, 2048), (2048, 4096), (4096, 4112)):
+        for a in range(0, 4112, 1024):
+            b = min(a + 1024, 4112)
             dsig(Y.dma_start(tb[:, a:b], T.zb[:, 0:b - a]), t_tb)
-
-    k1 = new()
-    sig(iota(T.cz[:, :], [[0, 2048]]), k1)
-    sig(iota(T.ones[:, :], [[0, 128]], 1), k1)
-    w("g", k1)
 
     def view(b, start):
         return T.cz[:, b + start:b + start + 113:16]
@@ -188,139 +190,121 @@ def rank_program(g, core, T, topo):
 
     def setw(x, pattern, wt, base, cm):
         return g.affine_select(x, x, pattern, A.is_ge, wt, base, cm)
-    k2, k3, k4, k5, k6 = new(), new(), new(), new(), new()
+    k2, k3, k4, k6 = new(), new(), new(), new()
     ep = T.cz[0:8, EP + 15:EP + 128:16]
-    sig(g.affine_select(ep, ep, [[-1, 8]], A.not_equal, 1.0, 0, 1), k2)
-    sig(put(view(Z1, 15), 0, 1.0), k2)
     grp = [[16, 8], [0, 16]]
     vx = view(ZX, 15)
-    for b, wt in ((OC, 0.5), (ON4, -2048.0), (FO, 1.0), (FT, 1.0)):
+    w("g", t_cz)
+    sig(g.affine_select(ep, ep, [[-1, 8]], A.not_equal, 1.0, 0, 1), k2)
+    sig(put(view(ZN, 15), 0, 1024.0), k3)
+    for b, wt in ((ON4, -2048.0), (FO, 1.0), (FT, 1.0)):
         sig(setw(cz(b), grp, wt, -1, -1), k3)
     sig(g.affine_select(cz(DG), cz(DG), [[-1, 128]], A.not_equal, 2048.0, 0, 1), k3)
     sig(setw(vx, [[16, 8]], 1.0, -1, -1), k3)
-    sig(put(view(ZS, 14), 0, 1.0), k3)
-    sig(put(view(ZS, 15), 1, 1.0), k3)
-    sig(put(view(ZN, 15), 0, 256.0), k3)
+    sig(put(view(FQ, 1), 7, 1.0), k3)
+    sig(put(view(Z1, 15), 0, 1.0), k3)
     sig(put(view(ZW, 15), 0, 256.0), k3)
     sig(put(view(FP, 1), 2, 1.0), k3)
-    sig(put(view(FN, 0), 0, 128.0), k3)
-    sig(put(view(FN, 1), 2, 1.0), k3)
+    sig(put(view(FN, 0), 4, 128.0), k3)
+    sig(put(view(FN, 1), 6, 1.0), k3)
     w("g", k3)
-    for b in (OC, ON4, FO):
+    sig(put(view(ZN, 15), 1, 1.0), k4)
+    for b in (ON4, FO):
         sig(setw(cz(b), grp, 0.0, 15, -1), k4)
     sig(setw(cz(FT), [[1, 128]], 0.0, 0, -1), k4)
     sig(setw(vx, [[16, 8]], 0.0, 15, -1), k4)
-    sig(put(view(ZN, 15), 1, 1.0), k4)
     sig(put(view(ZW, 15), 1, 1.0), k4)
-    sig(put(view(FP, 1), 3, 1.0), k4)
-    sig(put(view(FN, 0), 1, 1.0), k4)
-    w("g", k4)
-    sig(put(view(ZN, 15), 2, 16384.0), k5)
-    sig(iota(T.rc1[:, :], [[8, 32], [0, 8]], 1024), k5)
-    sig(iota(T.rc2[:, :], [[0, 32], [1, 8]]), k5)
-    sig(iota(T.cio[:, :], [[1, 256]]), k5)
-    sig(iota(T.mrow[:, :], [[1, 1024]], 2049), k6)
-    sig(iota(T.rw[:, :], [[16, 64]], 264, 1), k6)
+    sig(put(view(FN, 0), 5, 1.0), k4)
 
-    fm = new()
-    sig(S.activation(T.mk[:, 0:1024], T.zb[:, 0:1024], F.Copy), fm)
-    w("s", cu)
-    sig(S.activation(T.win[:, 0:264], T.zb[:, 0:264], F.Identity, bias=T.colF[:, :]), fm)
+    t_mk = sig(S.activation(T.mk[:, 0:1024], T.zb[:, :], F.Copy))
     w("p", t_pr8, k2)
     for kk in range(16):
         m = mm(ps[2][:, 0:256], cz(EP + 15 - kk, 128, 8), T.pr8[:, kk:4096:16], kk == 0, kk == 15)
     m_pt = sig(m)
     w("s", m_pt)
     c_pt = sig(S.activation(T.pt[:, :], ps[2][:, 0:256], F.Copy))
-    w("s", k4)
-    ksc = new()
-    sig(S.activation(view(ZL, 15), vx, F.Copy, scale=4096.0), ksc)
-    sig(S.activation(view(ZU, 15), vx, F.Copy, scale=T.colU[:, :]), ksc)
-    fnr = new()
-    sig(S.activation(T.nr[:, 0:2048], T.zb[:, :], F.Copy), fnr)
     w("g", c_pt)
     send(d1, T.lpt1[:, :], T.pt[:, :], "lpt1_s")
     send(d2, T.lpt2[:, :], T.pt[:, :], "lpt2_s")
-    w("y", c_pt)
-    t_ptd = dsig(Y.dma_start(T.ptd[:, :], T.pt[:, :]))
-    w("y", t_tb)
+    send(d3, T.lpt3[:, :], T.pt[:, :], "lpt3_s")
+    sig(iota(T.mrow[:, :], [[1, 1024]], 2049), k6)
+    sig(iota(T.rw[:, :], [[16, 64]], 264, 1), k6)
     tab1, tab2 = new(), new()
-    landed("y", "lpt1_s", n1)
+    w("y", t_tb)
+    landed("y", "lpt1_s", s1)
     dsig(Y.dma_start(T.tb1[2:128:16, 16:4112], T.lpt1[:, :]), tab1)
-    landed("y", "lpt2_s", n2)
+    landed("y", "lpt2_s", s2)
     dsig(Y.dma_start(T.tb2[2:128:16, 16:4112], T.lpt2[:, :]), tab2)
+    landed("y", "lpt3_s", s3)
+    dsig(Y.dma_start(T.tb1[7:128:16, 16:4112], T.lpt3[:, :]), tab1)
+    w("y", c_pt)
+    dsig(Y.dma_start(T.tb1[6:128:16, 16:4112], T.pt[:, :]), tab1)
 
     w("s", t_sc, c_nxt)
     w("v", t_sc, c_nxt)
-    gt = [None] * 4
-    for i in range(2):
-        for j in (i, i + 2):
-            o, src = T.gat[:, 1024 * j:1024 * j + 1024], T.tab[:, :].indirect(T.nxt_u[:, 64 * j:64 * j + 64])
-            gt[j] = sig(V.tensor_copy(o, src) if j < 2 else S.activation(o, src, F.Copy))
-    m_cd, m_hl = new(), [new(), new()]
-
-    def fold_code(j):
+    gt = []
+    for j in range(4):
+        o, src = T.gat[:, 1024 * j:1024 * j + 1024], T.tab[:, :].indirect(T.nxt_u[:, 64 * j:64 * j + 64])
+        gt.append(sig(V.tensor_copy(o, src) if j % 2 == 0 else S.activation(o, src, F.Copy)))
+    m_cd = [new(), new()]
+    w("p", k5)
+    mm(ps[3][:, 0:256], T.ones[:, :], T.rc1[:, :], True, False)
+    mm(ps[3][:, 0:256], T.ones[:, :], T.rc2[:, :], False, False)
+    w("p", k3, k4)
+    for j in range(4):
+        w("p", gt[j])
         for kk in range(16):
-            m = mm(ps[6][:, 64 * j:64 * j + 64], cz(ZN + 15 - kk), T.gat[:, 1024 * j + kk:1024 * j + 1024:16],
-                   kk == 0, kk == 15)
-        sig(m, m_cd)
+            m = mm(ps[6 + j // 2][:, 64 * (j % 2):64 * (j % 2) + 64], cz(ZN + 15 - kk),
+                   T.gat[:, 1024 * j + kk:1024 * j + 1024:16], kk == 0, kk == 15)
+        sig(m, m_cd[j // 2])
 
-    def fold_pair(j):
-        for hh in range(2):
-            for k in range(8):
-                m = mm(ps[hh][:, 64 * j:64 * j + 64], cz(ZS + 14 - 2 * k),
-                       T.gat[:, 1024 * j + 8 * hh + k:1024 * j + 1024:16], k == 0, k == 7)
-            sig(m, m_hl[hh])
-    w("p", k3, k4, k5)
-    for j in (0, 2):
-        w("p", gt[j])
-        fold_pair(j)
-    fold_code(0)
-    for j in (1, 3):
-        w("p", gt[j])
-        fold_pair(j)
-
-    zz, nm0, nm1 = new(), new(), new()
-    sig(V.memset(T.f0[:, 0:8], 0.0), zz)
-    sig(V.memset(T.f1[:, 0:8], 0.0), zz)
+    w("v", m_cd[0])
+    f_l, f_l0 = new(), new()
+    sig(V.tensor_scalar(T.fl[:, 8:136], ps[6][:, 0:128], 0.0, None, A.is_gt), f_l0)
+    nm0, nm1 = new(), new()
     sig(V.tensor_scalar(T.onh[:, :], T.own_i[:, :], 7, None, A.arith_shift_right), nm0)
     sig(V.tensor_scalar(T.onl[:, :], T.own_i[:, :], 127, None, A.bitwise_and), nm0)
-    w("v", m_hl[0])
-    f0 = sig(V.tensor_scalar(T.f0[:, 8:264], ps[0][:, 0:256], 0.0, None, A.is_gt))
-    w("s", m_hl[1])
-    f1 = sig(S.activation(T.f1[:, 8:264], ps[1][:, 0:256], F.Sign))
-    hlb = sig(S.activation(T.hl[:, 256:512], ps[1][:, 0:256], F.Copy))
-    hla = sig(V.tensor_copy(T.hl[:, 0:256], ps[0][:, 0:256]))
-    w("p", f0, f1, zz, c_pt, k1)
-    mm(ps[2][:, 0:256], cz(OC), T.f0[:, 7:263], True, False)
-    m_c = sig(mm(ps[2][:, 0:256], cz(OC), T.f1[:, 7:263], False, True))
-    mm(ps[3][:, 0:256], cz(ON4), T.f0[:, 8:264], True, False)
-    mm(ps[3][:, 0:256], cz(ON4), T.f1[:, 8:264], False, False)
-    mm(ps[3][:, 0:256], T.ones[:, :], T.rc1[:, :], False, False)
-    m_x = sig(mm(ps[3][:, 0:256], T.ones[:, :], T.rc2[:, :], False, True))
-    fold_code(2)
-    w("g", hla, hlb)
-    send(d1, T.lhl1[:, :], T.hl[:, :], "lhl1_s")
-    send(d2, T.lhl2[:, :], T.hl[:, :], "lhl2_s")
+    w("v", nm0)
+    sig(V.tensor_copy(T.nmb[:, 0:256], T.onh[:, :]), nm1)
+    w("v", m_cd[1])
+    sig(V.tensor_scalar(T.fl[:, 136:264], ps[7][:, 0:128], 0.0, None, A.is_gt), f_l)
+    w("p", f_l0, f_l, zz, c_pt)
+    m_c = sig(mm(ps[2][:, 0:256], cz(FO), T.fl[:, 7:263], True, True))
+    m_x = sig(mm(ps[3][:, 0:256], cz(ON4), T.fl[:, 8:264], False, True))
+    x1 = new()
+    for hh in range(2):
+        w("s", m_cd[hh], f_l if hh else f_l0)
+        sig(S.activation(T.hr[:, 128 * hh:128 * hh + 128], ps[6 + hh][:, 0:128], F.Identity, bias=MAGIC, scale=1.0 / 1024), x1)
     w("v", m_c, z0)
     ta = sig(V.tensor_tensor_scan(T.ax[:, :], ps[2][:, 0:256], T.zb[:, 0:256], 0.0, A.add, A.add))
-    w("v", k2)
+    w("v", k4)
     z1h = sig(V.tensor_copy(T.z1[:, :], cz(Z1, 144)))
     w("v", ta, m_x)
     to = sig(V.tensor_tensor(T.o16[:, :], T.ax[:, :], ps[3][:, 0:256], A.max))
+    w("s", x1)
+    c_p5 = sig(S.activation(T.p5[:, :], T.hr[:, :], F.Identity, bias=-1024.0 * MAGIC, scale=1024.0))
+    hlp = sig(S.activation(T.hl[:, 0:256], T.hr[:, :], F.Identity, bias=-MAGIC))
+    w("s", hlp)
+    c_p8 = sig(S.activation(T.p8[:, :], T.hl[:, 0:256], F.Identity, bias=2304.0, scale=768.0))
     w("p", z1h, to)
     for k in range(16):
         m = mm(ps[5][:, 0:16], T.z1[:, 15 - k:143 - k], T.o16[:, k:256:16], k == 0, k == 15)
     m_o = sig(m)
-    fold_code(1)
-    fold_code(3)
-    w("v", nm0)
-    sig(V.tensor_copy(T.nmb[:, 0:256], T.onh[:, :]), nm1)
+    mm(ps[4][:, 0:256], cz(FT), T.fl[:, 8:264], True, False)
+    m_p = sig(mm(ps[4][:, 0:256], cz(DG), T.fl[:, 8:264], False, True))
+    w("v", c_p5)
+    hlc = new()
+    for hh in range(2):
+        sig(V.tensor_tensor(T.hl[:, 256 + 128 * hh:384 + 128 * hh], ps[6 + hh][:, 0:128], T.p5[:, 128 * hh:128 * hh + 128],
+                            A.subtract), hlc)
+    zxh = sig(V.tensor_copy(T.zx[:, :], cz(ZX, 144)))
     sig(V.tensor_copy(T.nmb[:, 256:512], T.onl[:, :]), nm1)
-    sig(S.activation(T.nr[:, 2048:4096], T.zb[:, :], F.Copy), fnr)
+    w("g", hlp, hlc)
+    send(d1, T.lhl1[:, :], T.hl[:, :], "lhl1_s")
+    send(d2, T.lhl2[:, :], T.hl[:, :], "lhl2_s")
     w("v", m_o)
     tol = sig(V.tensor_copy(T.ol[:, :], ps[5][:, 0:16]))
-    w("v", tol, fm, k5)
+    w("v", tol, t_mk, k5)
     tmk = sig(V.tensor_copy(T.mk[:, :].indirect(T.ol[:, :]), T.cio[:, :]))
     w("v", tmk)
     tcm = sig(V.tensor_tensor_scan(T.cm[:, :], T.mk[:, 0:1024], T.zb[:, 0:1024], 0.0, A.max, A.max))
@@ -328,74 +312,60 @@ def rank_program(g, core, T, topo):
     for k in range(16):
         m = mm(ps[5][:, 64:128], cz(Z1 + 15 - k), T.cm[:, k:1024:16], k == 0, k == 15)
     m_l1 = sig(m)
-    w("s", m_cd)
-    x1 = sig(S.activation(T.hr[:, :], ps[6][:, 0:256], F.Identity, bias=MAGIC, scale=1.0 / 16384))
-    w("s", x1)
-    c_hp = sig(S.activation(T.hp[:, :], T.hr[:, :], F.Identity, bias=-MAGIC))
-    w("s", c_hp)
-    c_p8 = sig(S.activation(T.p8[:, :], T.hp[:, :], F.Identity, bias=2304.0, scale=16384.0))
-    w("g", c_hp)
-    send(d2, T.lhp[:, :], T.hp[:, :], "lhp_s")
-    w("v", x1)
-    fl = sig(V.tensor_scalar(T.fl[:, :], ps[6][:, 0:256], 0.0, None, A.is_gt))
-    sig(V.memset(T.fl4[:, 0:8], 0.0), zz)
-    w("p", fl)
-    mm(ps[4][:, 0:256], cz(FT), T.fl[:, :], True, False)
-    m_p = sig(mm(ps[4][:, 0:256], cz(DG), T.fl[:, :], False, True))
     for k in range(16):
-        mm(ps[7][:, 0:64], cz(Z1 + 15 - k), T.cm[:, k:1024:16], k == 0, False)
-    w("y", nm1)
-    t_nmd = dsig(Y.dma_start(T.nmd[:, :], T.nmb[:, :]))
-    t_nr = new()
-    w("s", fnr, t_nmd, t_ptd)
-    dsig(S.dma_start(T.nr[0:128:16, :], T.nmd[:, 0:256]), t_nr)
-    dsig(S.dma_start(T.nr[1:128:16, :], T.nmd[:, 256:512]), t_nr)
-    dsig(S.dma_start(T.nr[2:128:16, :], T.ptd[:, :]), t_nr)
-    for tb, ld, sm, cnt, tk in ((T.tb1, T.lhl1, "lhl1_s", n1, tab1), (T.tb2, T.lhl2, "lhl2_s", n2, tab2)):
-        landed("y", sm, cnt)
-        for s_ in range(2):
-            for hh in range(2):
-                dsig(Y.dma_start(tb[s_:128:16, 16 + 2048 * hh:2064 + 2048 * hh], ld[s_:128:2, 256 * hh:256 * hh + 256]), tk)
-    landed("y", "lhp_s", n2)
-    dsig(Y.dma_start(T.tb2[3:128:16, 16:4112], T.lhp[:, :]), tab2)
-
-    w("v", m_l1)
-    tl1 = sig(V.tensor_copy(T.l1[:, :], ps[5][:, 64:128]))
+        mm(ps[2][:, 0:64], cz(Z1 + 15 - k), T.cm[:, k:1024:16], k == 0, False)
     w("v", m_p)
     twq = sig(V.tensor_tensor(T.wq[:, :], T.ax[:, :], ps[4][:, 0:256], A.add))
+    w("v", c_p8)
+    tcd = new()
+    for hh in range(2):
+        sig(V.tensor_tensor(T.cd[:, 128 * hh:128 * hh + 128], ps[6 + hh][:, 0:128], T.p8[:, 128 * hh:128 * hh + 128],
+                            A.subtract), tcd)
+    w("v", m_l1)
+    tl1 = sig(V.tensor_copy(T.l1[:, :], ps[5][:, 64:128]))
     w("v", tl1, twq, k6)
     tse = sig(V.tensor_tensor(T.sel[:, :], T.wq[:, :].indirect(T.l1[:, :]), T.mrow[:, :], A.is_equal))
-    w("v", c_p8)
-    tcd = sig(V.tensor_tensor(T.cd[:, :], ps[6][:, 0:256], T.p8[:, :], A.subtract))
-    w("v", k4)
-    zxh = sig(V.tensor_copy(T.zx[:, :], cz(ZX, 144)))
-    w("v", tse, tcd)
-    ths = sig(V.tensor_tensor(T.hls[:, :], T.cd[:, :].indirect(T.l1[:, :]), T.sel[:, :], A.mult))
+    w("s", nm1, t_tb)
+    dsig(S.dma_start(T.tb1[4:128:16, 16:4112], T.nmb[:, 0:256]), tab1)
+    dsig(S.dma_start(T.tb1[5:128:16, 16:4112], T.nmb[:, 256:512]), tab1)
+    for tb, ld, sm, src, tk in ((T.tb1, T.lhl1, "lhl1_s", s1, tab1), (T.tb2, T.lhl2, "lhl2_s", s2, tab2)):
+        landed("y", sm, src)
+        for s_ in range(2):
+            dsig(Y.dma_start(tb[s_:128:16, 16:4112], ld[:, 256 * s_:256 * s_ + 256]), tk)
+
+    w("s", k4, cu)
+    ksc, fw = new(), new()
+    sig(S.activation(view(ZL, 15), vx, F.Copy, scale=4096.0), ksc)
+    sig(S.activation(view(ZU, 15), vx, F.Copy, scale=T.colU[:, :]), ksc)
+    sig(S.activation(T.win[:, 0:264], T.zb[:, 0:264], F.Identity, bias=T.colF[:, :]), fw)
     w("p", tse, ksc)
     for k in range(16):
-        mm(ps[5][:, 128:192], cz(ZL + 15 - k), T.sel[:, k:1024:16], k == 0, False)
-    for k in range(16):
-        m = mm(ps[7][:, 0:64], cz(ZU + 15 - k), T.sel[:, k:1024:16], False, k == 15)
+        m = mm(ps[2][:, 0:64], cz(ZU + 15 - k), T.sel[:, k:1024:16], False, k == 15)
     m_lo = sig(m)
+    for k in range(16):
+        mm(ps[5][:, 128:192], cz(ZL + 15 - k), T.sel[:, k:1024:16], k == 0, False)
+    w("v", tse, tcd)
+    ths = sig(V.tensor_tensor(T.hls[:, :], T.cd[:, :].indirect(T.l1[:, :]), T.sel[:, :], A.mult))
     w("p", ths, zxh)
     for k in range(16):
         m = mm(ps[5][:, 128:192], T.zx[:, 15 - k:143 - k], T.hls[:, k:1024:16], False, k == 15)
     m_l2 = sig(m)
+    tll = new()
     w("v", m_lo)
-    tlo = sig(V.tensor_copy(T.lo[:, :], ps[7][:, 0:64]))
+    sig(V.tensor_scalar(T.ll[:, 64:128], ps[2][:, 0:64], 16.0, None, A.add), tll)
     w("v", m_l2)
-    tl2 = sig(V.tensor_scalar(T.l2[:, :], ps[5][:, 128:192], -2033.0, None, A.add))
+    sig(V.tensor_scalar(T.ll[:, 0:64], ps[5][:, 128:192], -2033.0, None, A.add), tll)
 
-    def pick(tb, lst, out, toks):
+    def pick(tb, lst, at, cut, out, toks):
         ts = []
-        for q, sl, ll in (("v", slice(0, 512), slice(0, 32)), ("s", slice(512, 1024), slice(32, 64))):
+        for q, u, v in (("v", 0, cut), ("s", cut, 64)):
             w(q, *toks)
-            src = tb[:, :].indirect(lst[:, ll])
-            ts.append(sig(V.tensor_copy(out[:, sl], src) if q == "v" else S.activation(out[:, sl], src, F.Copy)))
+            src, o = tb[:, :].indirect(lst[:, at + u:at + v]), out[:, 16 * u:16 * v]
+            ts.append(sig(V.tensor_copy(o, src) if q == "v" else S.activation(o, src, F.Copy)))
         return ts
-    tr1 = pick(T.tb1, T.l2, T.r1, [tl2, tab1])
-    tng = pick(T.nr, T.lo, T.ng, [tlo, t_nr])
-    w("p", hlb, tcd, tlo, *tr1)
+    tr1 = pick(T.tb1, T.ll, 0, 32, T.r1, [tll, tab1])
+    tng = pick(T.tb1, T.ll, 64, NG, T.ng, [tll])
+    w("p", tcd, tll, *tr1)
     for k in range(16):
         m = mm(ps[1][:, 0:64], cz(ZW + 15 - k), T.r1[:, k:1024:16], k == 0, k == 15)
     m_l3 = sig(m)
@@ -403,39 +373,51 @@ def rank_program(g, core, T, topo):
         mm(ps[6 + hh][:, :], cz(FP), T.r1[:, 512 * hh:512 * hh + 512], True, False)
     w("v", m_l3)
     tl3 = sig(V.tensor_scalar(T.l3[:, :], ps[1][:, 0:64], -241.0, None, A.add))
-    tr2 = pick(T.tb2, T.l3, T.r2, [tl3, tab2])
+    tr2 = pick(T.tb2, T.l3, 0, 32, T.r2, [tl3, tab2])
+    w("p", *tng)
     for hh in range(2):
-        w("p", tng[hh])
         mm(ps[6 + hh][:, :], cz(FN), T.ng[:, 512 * hh:512 * hh + 512], False, False)
     w("p", *tr2)
     for k in range(16):
-        m = mm(ps[1][:, 64:128], cz(ZW + 15 - k), T.r2[:, k:1024:16], k == 0, k == 15)
+        m = mm(ps[0][:, 256:320], cz(ZW + 15 - k), T.r2[:, k:1024:16], k == 0, k == 15)
     m_l4 = sig(m)
-    m_fd = [sig(mm(ps[6][:, :], cz(FP), T.r2[:, 0:512], False, True))]
+    for hh in range(2):
+        mm(ps[6 + hh][:, :], cz(FP), T.r2[:, 512 * hh:512 * hh + 512], False, False)
 
     w("v", m_l4)
-    f4 = sig(V.tensor_scalar(T.fl4[:, 8:72], ps[1][:, 64:128], 0.0, None, A.is_gt))
-    x1 = sig(V.tensor_scalar(T.xn[:, :], ps[1][:, 64:128], 0.0, -4096.0, A.is_gt, A.mult))
+    tl5 = sig(V.tensor_scalar(T.l5[:, :], ps[0][:, 256:320], -241.0, None, A.add))
+    w("s", tl5)
+    tr3 = [sig(S.activation(T.r3[:, 512 * hh:512 * hh + 512], T.tb1[:, :].indirect(T.l5[:, 32 * hh:32 * hh + 32]), F.Copy))
+           for hh in range(2)]
+    f4 = sig(V.tensor_scalar(T.fl4[:, 8:72], ps[0][:, 256:320], 0.0, None, A.is_gt))
+    x2 = sig(V.tensor_scalar(T.xn[:, :], ps[0][:, 256:320], 0.0, -4096.0, A.is_gt, A.mult))
     w("p", f4, zz)
     m_a = sig(mm(ps[2][:, 0:64], cz(FO), T.fl4[:, 7:71], True, True))
     m_q = sig(mm(ps[3][:, 0:64], cz(FT), T.fl4[:, 8:72], True, True))
-    m_fd.append(sig(mm(ps[7][:, :], cz(FP), T.r2[:, 512:1024], False, True)))
-    w("v", x1)
-    x2 = sig(V.tensor_tensor(T.xx[:, :], T.xn[:, :], T.rw[:, :], A.add))
-    tfd = []
+    m_fd = []
     for hh in range(2):
-        w("s", m_fd[hh])
-        tfd.append(sig(S.activation(T.fd[:, 512 * hh:512 * hh + 512], ps[6 + hh][:, :], F.Copy)))
+        w("p", tr3[hh])
+        m_fd.append(sig(mm(ps[6 + hh][:, :], cz(FQ), T.r3[:, 512 * hh:512 * hh + 512], False, True)))
+    w("v", x2, k6)
+    x3 = sig(V.tensor_tensor(T.xx[:, :], T.xn[:, :], T.rw[:, :], A.add))
     w("v", m_a)
     q1 = sig(V.tensor_tensor_scan(T.a4[:, :], ps[2][:, 0:64], T.zb[:, 0:64], 0.0, A.add, A.add))
     w("v", q1, m_q)
     q2 = sig(V.tensor_tensor(T.q4[:, :], T.a4[:, :], ps[3][:, 0:64], A.add))
-    w("v", q2, x2)
+    w("v", q2, x3)
     q3 = sig(V.tensor_tensor(T.o4[:, :], T.q4[:, :], T.xx[:, :], A.max))
     w("v", q3)
     q5 = sig(V.tensor_copy(T.l4[:, :], T.o4[:, :]))
-    w("v", q5, *tfd)
-    tw = sig(V.tensor_copy(T.win[:, :].indirect(T.l4[:, :]), T.fd[:, :]))
+    w("v", m_fd[0])
+    w("s", m_fd[1])
+    tfd = [sig(V.tensor_copy(T.fd[:, 0:512], ps[6][:, :])), sig(S.activation(T.fd[:, 512:1024], ps[7][:, :], F.Copy))]
+    w("v", q5, fw)
+    tw = None
+    for hh in range(2):
+        w("v", tfd[hh])
+        if tw:
+            w("v", tw)
+        tw = sig(V.tensor_copy(T.win[:, :].indirect(T.l4[:, 32 * hh:32 * hh + 32]), T.fd[:, 512 * hh:512 * hh + 512]))
     w("y", tw)
     t_y = new()
     w("s", tw)

@@ -4,31 +4,33 @@ BF, F32, F16, I32, U16 = "bfloat16", "float32", "float16", "int32", "uint16"
 SCRATCH = {
     "own_i": ("sbuf", [128, 256], I32), "nxt_i": ("sbuf", [128, 256], I32), "pts_i": ("sbuf", [128, 256], I32),
     "own_u": ("sbuf", [128, 256], U16), "nxt_u": ("sbuf", [128, 256], U16), "own_r": ("sbuf", [128, 256], U16),
-    "onh": ("sbuf", [128, 256], I32), "onl": ("sbuf", [128, 256], I32), "nmb": ("sbuf", [128, 512], BF),
-    "ptsb": ("sbuf", [128, 256], BF), "zb": ("sbuf", [128, 1024], BF),
+    "onh": ("sbuf", [128, 256], BF), "nmb": ("sbuf", [128, 512], BF),
+    "ptsb": ("sbuf", [128, 256], BF), "zb": ("sbuf", [128, 1028], BF),
     "tab": ("sbuf", [128, 16384], BF), "dat": ("sbuf", [128, 4096], BF), "gat": ("sbuf", [128, 4096], BF),
     "pidx": ("sbuf", [128, 1], I32), "par": ("sbuf", [128, 1], I32), "p16": ("sbuf", [128, 1], I32),
     "colA": ("sbuf", [128, 1], F32), "colB": ("sbuf", [128, 1], F32), "colF": ("sbuf", [128, 1], F32),
-    "colU": ("sbuf", [128, 1], F32), "lb0": ("sbuf", [128, 16], F32), "lb": ("sbuf", [128, 16], F32),
+    "colU": ("sbuf", [128, 1], F32), "colN": ("sbuf", [128, 1], F32), "totm": ("sbuf", [128, 1], F32),
+    "lb0": ("sbuf", [128, 16], F32), "lb": ("sbuf", [128, 16], F32),
     "bl": ("sbuf", [128, 256], BF), "bh": ("sbuf", [128, 256], BF), "bx": ("sbuf", [128, 256], BF),
     "by": ("sbuf", [128, 256], BF), "bs": ("sbuf", [128, 256], BF),
-    "cz": ("sbuf", [128, 2048], BF),
-    "z1": ("sbuf", [128, 144], F16), "zx": ("sbuf", [128, 144], F16), "ones": ("sbuf", [1, 128], BF),
-    "rc1": ("sbuf", [1, 256], BF), "rc2": ("sbuf", [1, 256], BF),
+    "cz": ("sbuf", [128, 2176], BF),
+    "z1": ("sbuf", [128, 144], F16), "zx": ("sbuf", [128, 144], F16), "t32": ("sbuf", [1, 256], BF),
+    "c32": ("sbuf", [1, 256], BF),
     "mrow": ("sbuf", [128, 1024], F32), "cio": ("sbuf", [128, 256], BF), "rw": ("sbuf", [128, 64], F32),
+    "sl": ("sbuf", [128, 64], F32), "tk": ("sbuf", [128, 64], F32), "thr": ("sbuf", [128, 64], F32),
     "mk": ("sbuf", [128, 1280], BF), "pr8": ("sbuf", [8, 4096], BF), "pt": ("sbuf", [128, 256], BF),
-    "ng": ("sbuf", [128, 1024], BF), "hl": ("sbuf", [128, 512], BF), "hr": ("sbuf", [128, 256], F32),
-    "p5": ("sbuf", [128, 256], F32), "p8": ("sbuf", [128, 256], F32), "cd": ("sbuf", [128, 256], F32),
+    "ng": ("sbuf", [128, 1024], BF), "hl": ("sbuf", [128, 512], BF),
+    "p5": ("sbuf", [128, 256], F32), "cd": ("sbuf", [128, 256], F32),
     "fl": ("sbuf", [128, 264], BF),
-    "ax": ("sbuf", [128, 256], F32), "o16": ("sbuf", [128, 256], F16), "wq": ("sbuf", [128, 256], F32),
+    "ax": ("sbuf", [128, 257], F32), "o16": ("sbuf", [128, 256], F16), "wq": ("sbuf", [128, 256], F32),
     "ol": ("sbuf", [128, 16], U16), "cm": ("sbuf", [128, 1024], BF), "l1": ("sbuf", [128, 64], U16),
     "sel": ("sbuf", [128, 1024], BF), "hls": ("sbuf", [128, 1024], F16),
     "ll": ("sbuf", [128, 128], U16), "l3": ("sbuf", [128, 64], U16), "l4": ("sbuf", [128, 64], U16),
     "l5": ("sbuf", [128, 64], U16),
     "tb1": ("sbuf", [128, 4112], BF), "tb2": ("sbuf", [128, 4112], BF),
-    "r1": ("sbuf", [128, 1024], BF), "r2": ("sbuf", [128, 1024], BF), "r3": ("sbuf", [128, 1024], BF),
+    "r1": ("sbuf", [128, 1024], BF), "r2": ("sbuf", [128, 1024], BF), "r3": ("sbuf", [128, 1024], F32),
     "fl4": ("sbuf", [128, 72], BF), "xn": ("sbuf", [128, 64], F32), "xx": ("sbuf", [128, 64], F32),
-    "a4": ("sbuf", [128, 64], F32), "q4": ("sbuf", [128, 64], F32), "o4": ("sbuf", [128, 64], F32),
+    "a4": ("sbuf", [128, 64], F32), "o4": ("sbuf", [128, 64], F32),
     "fd": ("sbuf", [128, 1024], F32), "win": ("sbuf", [128, 1408], F32),
     "lpt1": ("dram", [128, 256], BF), "lpt2": ("dram", [128, 256], BF), "lpt3": ("dram", [128, 256], BF),
     "lhl1": ("dram", [128, 512], BF), "lhl2": ("dram", [128, 512], BF),
@@ -38,12 +40,14 @@ for _b in range(8):
 NE = 138
 SEMAPHORES = ["own_r_s", "lpt1_s", "lpt2_s", "lpt3_s", "lhl1_s", "lhl2_s", "ls"] + ["e%d" % _i for _i in range(NE)]
 
-ZW, ZN, EP, Z1, ZX, ZL, ZU = 144, 288, 432, 576, 720, 864, 1008
-ON4, DG, FO, FT, FP, FN, FQ = 1152, 1280, 1408, 1536, 1664, 1792, 1920
-MAGIC = 12582912.0
-TG, TD, TS = 768, 2048, 5632
+I1, I256 = 0, 2048
+ZW, ZN, EP, Z1, ZX, ZU = 144, 288, 432, 576, 720, 864
+FS, ON4, DG, FO, FT, FP, FN, FR = 1024, 1152, 1280, 1408, 1536, 1664, 1792, 1920
+TG0, TG, TD, TS = 384, 1408, 2048, 6656
 AE = 1536
-NG = 28
+N0, N1, R1, R2 = 20, 36, 36, 36
+B0 = 192.0
+BW = 256.0 * B0
 
 
 def rank_program(g, core, T, topo):
@@ -105,22 +109,23 @@ def rank_program(g, core, T, topo):
     t_pts = dsig(Y.dma_start(T.pts_i[:, :], T.pts[:, :]))
 
     k0, k1, k5 = new(), new(), new()
+    f_tab, f_tabv, t_tab, t_cz = new(), new(), new(), new()
     sig(g.iota(T.pidx[:, :], [[0, 1]], 0, 1), k0)
     sig(iota(T.lb0[:, :], [[16, 16]]), k0)
     sig(iota(T.bl[:, :], [[1, 16], [0, 16]]), k1)
     sig(iota(T.bh[:, :], [[0, 16], [1, 16]]), k1)
+    sig(iota(T.tab[:, 0:TG0], [[0, TG0]]), f_tab)
 
     z0 = sig(V.memset(T.zb[:, :], 0.0))
     w("s", z0)
-    f_tab, f_tabv, t_tab, t_cz = new(), new(), new(), new()
     for a in range(TG + TD, TG + TD + TS, 1024):
         b = min(a + 1024, TG + TD + TS)
         sig(S.activation(T.tab[:, a:b], T.zb[:, 0:b - a], F.Copy), f_tab)
     w("y", z0)
     for a in range(TG, TG + TD, 1024):
-        dsig(Y.dma_start(T.tab[:, a:a + 1024], T.zb[:, :]), t_tab)
+        dsig(Y.dma_start(T.tab[:, a:a + 1024], T.zb[:, 0:1024]), t_tab)
     for a in (0, 1024):
-        dsig(Y.dma_start(T.cz[:, a:a + 1024], T.zb[:, :]), t_cz)
+        dsig(Y.dma_start(T.cz[:, a:a + 1024], T.zb[:, 0:1024]), t_cz)
     V0 = TG + TD + TS
     VE = V0 + 2048
     sig(V.memset(T.tab[:, V0:VE], 0.0), f_tabv)
@@ -150,23 +155,17 @@ def rank_program(g, core, T, topo):
     w("v", t_nxt)
     c_nxt = sig(V.tensor_copy(T.nxt_u[:, :], T.nxt_i[:, :]))
     sig(V.memset(T.tab[:, VE:16384], 0.0), f_tabv)
-    cu = new()
-    sig(V.tensor_scalar(T.colF[:, :], T.p16[:, :], 0, -1.0, A.is_equal, A.mult), cu)
-    sig(V.tensor_scalar(T.colU[:, :], T.p16[:, :], 256.0, None, A.mult), cu)
     w("s", b1, b2)
     for ch in range(AE // 256, 16):
         sig(S.activation(T.dat[:, 256 * ch:256 * ch + 256], T.bs[:, :], F.Identity, bias=T.lb[:, ch:ch + 1]), db)
 
     w("g", c_own)
     send(d1, T.own_r[:, :], T.own_u[:, :], "own_r_s")
-    sig(iota(T.ones[:, :], [[0, 128]], 1), k5)
-    sig(iota(T.rc1[:, :], [[8, 32], [0, 8]], 1024), k5)
-    sig(iota(T.rc2[:, :], [[0, 32], [1, 8]]), k5)
+    sig(iota(T.tab[:, TG0:TG], [[0, TG - TG0]]), f_tab)
     sig(iota(T.cio[:, :], [[1, 256]]), k5)
-    zz = new()
-    sig(iota(T.tab[:, 0:TG], [[0, TG]]), f_tab)
-    sig(iota(T.fl[:, 0:8], [[0, 8]]), zz)
-    sig(iota(T.fl4[:, 0:8], [[0, 8]]), zz)
+    k6, km, ks, zz = new(), new(), new(), new()
+    sig(iota(T.mrow[:, 0:128], [[1, 128]], 2049), km)
+    sig(iota(T.rw[:, :], [[16, 64]], 264, 1), k6)
 
     w("v", f_tab, f_tabv, t_tab, da)
     landed("v", "own_r_s", s1)
@@ -178,9 +177,8 @@ def rank_program(g, core, T, topo):
     t_pr8 = dsig(Y.dma_start(T.pr8[:, :], T.ptsb[:, :]))
     t_tb = new()
     for tb in (T.tb1, T.tb2):
-        for a in range(0, 4112, 1024):
-            b = min(a + 1024, 4112)
-            dsig(Y.dma_start(tb[:, a:b], T.zb[:, 0:b - a]), t_tb)
+        for a in range(0, 4112, 1028):
+            dsig(Y.dma_start(tb[:, a:a + 1028], T.zb[:, :]), t_tb)
 
     def view(b, start):
         return T.cz[:, b + start:b + start + 113:16]
@@ -190,67 +188,87 @@ def rank_program(g, core, T, topo):
 
     def setw(x, pattern, wt, base, cm):
         return g.affine_select(x, x, pattern, A.is_ge, wt, base, cm)
-    k2, k3, k4, k6 = new(), new(), new(), new()
+    k2, k3, k4, kf, kz = new(), new(), new(), new(), new()
     ep = T.cz[0:8, EP + 15:EP + 128:16]
     grp = [[16, 8], [0, 16]]
     vx = view(ZX, 15)
     w("g", t_cz)
     sig(g.affine_select(ep, ep, [[-1, 8]], A.not_equal, 1.0, 0, 1), k2)
-    sig(put(view(ZN, 15), 0, 1024.0), k3)
-    for b, wt in ((ON4, -2048.0), (FO, 1.0), (FT, 1.0)):
-        sig(setw(cz(b), grp, wt, -1, -1), k3)
-    sig(g.affine_select(cz(DG), cz(DG), [[-1, 128]], A.not_equal, 2048.0, 0, 1), k3)
-    sig(setw(vx, [[16, 8]], 1.0, -1, -1), k3)
-    sig(put(view(FQ, 1), 7, 1.0), k3)
+    sig(put(view(ZN, 15), 0, 1024.0), kz)
+    w("g", kz)
+    sig(put(view(ZN, 15), 1, 1.0), kz)
+    sig(setw(cz(FO), grp, 1.0, -1, -1), kf)
+    w("g", kf)
+    sig(setw(cz(FO), grp, 0.0, 15, -1), kf)
     sig(put(view(Z1, 15), 0, 1.0), k3)
+    sig(setw(vx, [[16, 8]], 1.0, -1, -1), k3)
     sig(put(view(ZW, 15), 0, 256.0), k3)
-    sig(put(view(FP, 1), 2, 1.0), k3)
-    sig(put(view(FN, 0), 4, 128.0), k3)
-    sig(put(view(FN, 1), 6, 1.0), k3)
+    sig(put(view(FN, 8), 4, 128.0), k3)
+    w("g", kf)
+    sig(g.affine_select(cz(FT), cz(FO), [[1, 128]], A.is_ge, 0.0, 0, -1), k4)
+    sig(g.affine_select(cz(FS), cz(FO), [[-1, 128]], A.is_gt, 0.0, 0, 1), k4)
+    ki = sig(g.affine_select(cz(I1), cz(I1), [[-1, 128]], A.not_equal, 1.0, 0, 1))
+    sig(put(view(FP, 9), 2, 1.0), k4)
+    sig(put(view(FR, 9), 9, 1.0), k4)
+    sig(put(view(FN, 9), 6, 1.0), k4)
     w("g", k3)
-    sig(put(view(ZN, 15), 1, 1.0), k4)
-    for b in (ON4, FO):
-        sig(setw(cz(b), grp, 0.0, 15, -1), k4)
-    sig(setw(cz(FT), [[1, 128]], 0.0, 0, -1), k4)
     sig(setw(vx, [[16, 8]], 0.0, 15, -1), k4)
     sig(put(view(ZW, 15), 1, 1.0), k4)
-    sig(put(view(FN, 0), 5, 1.0), k4)
+    sig(put(view(FN, 8), 5, 1.0), k4)
 
-    t_mk = sig(S.activation(T.mk[:, 0:1024], T.zb[:, :], F.Copy))
+    kr = new()
+    sig(S.activation(T.t32[:, :], T.zb[0:1, 0:256], F.Identity, bias=32.0), kr)
+    sig(S.activation(T.fl[:, 0:8], T.zb[:, 0:8], F.Copy), zz)
+    sig(S.activation(T.fl4[:, 0:8], T.zb[:, 0:8], F.Copy), zz)
+    w("s", k5)
+    sig(S.activation(T.c32[:, :], T.cio[0:1, :], F.Copy, scale=1.0 / 32), kr)
+    for b in (128, 256, 512):
+        w("s", km)
+        sig(S.activation(T.mrow[:, b:2 * b], T.mrow[:, 0:b], F.Identity, bias=float(b)), km)
+    w("s", km)
+    sig(S.activation(T.sl[:, :], T.mrow[:, 0:1024:16], F.Identity, bias=-2049.0), ks)
     w("p", t_pr8, k2)
     for kk in range(16):
         m = mm(ps[2][:, 0:256], cz(EP + 15 - kk, 128, 8), T.pr8[:, kk:4096:16], kk == 0, kk == 15)
     m_pt = sig(m)
     w("s", m_pt)
     c_pt = sig(S.activation(T.pt[:, :], ps[2][:, 0:256], F.Copy))
+    w("s", kf)
+    sig(S.activation(cz(ON4), cz(FO), F.Copy, scale=-2048.0), kr)
+    w("s", ki)
+    sig(S.activation(cz(DG), cz(I1), F.Copy, scale=2048.0), kr)
+    sig(S.activation(cz(I256), cz(I1), F.Copy, scale=256.0), kr)
     w("g", c_pt)
     send(d1, T.lpt1[:, :], T.pt[:, :], "lpt1_s")
     send(d2, T.lpt2[:, :], T.pt[:, :], "lpt2_s")
     send(d3, T.lpt3[:, :], T.pt[:, :], "lpt3_s")
-    sig(iota(T.mrow[:, :], [[1, 1024]], 2049), k6)
-    sig(iota(T.rw[:, :], [[16, 64]], 264, 1), k6)
-    tab1, tab2 = new(), new()
+    t_mk = sig(iota(T.mk[:, 0:1024], [[0, 1024]]))
+    tab0, tab1, tab2 = new(), new(), new()
+    w("y", c_pt, t_sc)
+    dsig(Y.dma_start(T.dat[6:128:16, :], T.pt[:, :]), tab0)
     w("y", t_tb)
     landed("y", "lpt1_s", s1)
     dsig(Y.dma_start(T.tb1[2:128:16, 16:4112], T.lpt1[:, :]), tab1)
     landed("y", "lpt2_s", s2)
-    dsig(Y.dma_start(T.tb2[2:128:16, 16:4112], T.lpt2[:, :]), tab2)
+    dsig(Y.dma_start(T.tb2[9:128:16, 16:4112], T.lpt2[:, :]), tab2)
     landed("y", "lpt3_s", s3)
-    dsig(Y.dma_start(T.tb1[7:128:16, 16:4112], T.lpt3[:, :]), tab1)
-    w("y", c_pt)
-    dsig(Y.dma_start(T.tb1[6:128:16, 16:4112], T.pt[:, :]), tab1)
+    dsig(Y.dma_start(T.tb1[9:128:16, 16:4112], T.lpt3[:, :]), tab1)
 
     w("s", t_sc, c_nxt)
     w("v", t_sc, c_nxt)
     gt = []
     for j in range(4):
-        o, src = T.gat[:, 1024 * j:1024 * j + 1024], T.tab[:, :].indirect(T.nxt_u[:, 64 * j:64 * j + 64])
-        gt.append(sig(V.tensor_copy(o, src) if j % 2 == 0 else S.activation(o, src, F.Copy)))
+        t = new()
+        for hh in range(2):
+            a = 1024 * j + 512 * hh
+            o, src = T.gat[:, a:a + 512], T.tab[:, :].indirect(T.nxt_u[:, a // 16:a // 16 + 32])
+            sig(S.activation(o, src, F.Copy) if hh else V.tensor_copy(o, src), t)
+        gt.append(t)
     m_cd = [new(), new()]
-    w("p", k5)
-    mm(ps[3][:, 0:256], T.ones[:, :], T.rc1[:, :], True, False)
-    mm(ps[3][:, 0:256], T.ones[:, :], T.rc2[:, :], False, False)
-    w("p", k3, k4)
+    w("p", kr)
+    mm(ps[3][:, 0:256], T.t32[:, 0:128], T.t32[:, :], True, False)
+    mm(ps[3][:, 0:256], T.t32[:, 0:128], T.c32[:, :], False, False)
+    w("p", kz)
     for j in range(4):
         w("p", gt[j])
         for kk in range(16):
@@ -261,47 +279,59 @@ def rank_program(g, core, T, topo):
     w("v", m_cd[0])
     f_l, f_l0 = new(), new()
     sig(V.tensor_scalar(T.fl[:, 8:136], ps[6][:, 0:128], 0.0, None, A.is_gt), f_l0)
-    nm0, nm1 = new(), new()
-    sig(V.tensor_scalar(T.onh[:, :], T.own_i[:, :], 7, None, A.arith_shift_right), nm0)
-    sig(V.tensor_scalar(T.onl[:, :], T.own_i[:, :], 127, None, A.bitwise_and), nm0)
-    w("v", nm0)
-    sig(V.tensor_copy(T.nmb[:, 0:256], T.onh[:, :]), nm1)
+    hlc, x1, c_p5, nm1 = new(), new(), new(), new()
+    nm0 = sig(V.tensor_scalar(T.onh[:, :], T.own_i[:, :], 1.0 / 128, 128.0, A.mult, A.add))
+
+    def first(hh, fl_):
+        w("s", m_cd[hh], fl_)
+        x = sig(S.activation(T.hl[:, 128 * hh:128 * hh + 128], ps[6 + hh][:, 0:128], F.Identity, bias=B0, scale=1.0 / 1024), x1)
+        w("s", x)
+        sig(S.activation(T.p5[:, 128 * hh:128 * hh + 128], T.hl[:, 128 * hh:128 * hh + 128], F.Identity, bias=-1024.0 * B0,
+                         scale=1024.0), c_p5)
+
+    def second(hh):
+        w("v", c_p5)
+        sig(V.tensor_tensor(T.hl[:, 256 + 128 * hh:384 + 128 * hh], ps[6 + hh][:, 0:128], T.p5[:, 128 * hh:128 * hh + 128],
+                            A.subtract), hlc)
+    first(0, f_l0)
+    second(0)
+    w("s", nm0)
+    n128 = sig(S.activation(ps[1][:, 0:256], T.onh[:, :], F.Identity, bias=-16384.0, scale=128.0))
     w("v", m_cd[1])
     sig(V.tensor_scalar(T.fl[:, 136:264], ps[7][:, 0:128], 0.0, None, A.is_gt), f_l)
-    w("p", f_l0, f_l, zz, c_pt)
-    m_c = sig(mm(ps[2][:, 0:256], cz(FO), T.fl[:, 7:263], True, True))
-    m_x = sig(mm(ps[3][:, 0:256], cz(ON4), T.fl[:, 8:264], False, True))
-    x1 = new()
-    for hh in range(2):
-        w("s", m_cd[hh], f_l if hh else f_l0)
-        sig(S.activation(T.hr[:, 128 * hh:128 * hh + 128], ps[6 + hh][:, 0:128], F.Identity, bias=MAGIC, scale=1.0 / 1024), x1)
-    w("v", m_c, z0)
-    ta = sig(V.tensor_tensor_scan(T.ax[:, :], ps[2][:, 0:256], T.zb[:, 0:256], 0.0, A.add, A.add))
-    w("v", k4)
+    w("v", k3)
     z1h = sig(V.tensor_copy(T.z1[:, :], cz(Z1, 144)))
+    first(1, f_l)
+    sig(S.activation(T.nmb[:, 0:256], T.onh[:, :], F.Identity, bias=-128.0), nm1)
+    w("p", f_l0, f_l, zz, c_pt, kf, k3, k4)
+    m_c = sig(mm(ps[2][:, 0:257], cz(FO), T.fl[:, 7:264], True, True))
+    m_x = sig(mm(ps[3][:, 0:256], cz(ON4), T.fl[:, 8:264], False, True))
+    w("v", m_c, z0)
+    ta = sig(V.tensor_tensor_scan(T.ax[:, :], ps[2][:, 0:257], T.zb[:, 0:257], 0.0, A.add, A.add))
     w("v", ta, m_x)
-    to = sig(V.tensor_tensor(T.o16[:, :], T.ax[:, :], ps[3][:, 0:256], A.max))
-    w("s", x1)
-    c_p5 = sig(S.activation(T.p5[:, :], T.hr[:, :], F.Identity, bias=-1024.0 * MAGIC, scale=1024.0))
-    hlp = sig(S.activation(T.hl[:, 0:256], T.hr[:, :], F.Identity, bias=-MAGIC))
-    w("s", hlp)
-    c_p8 = sig(S.activation(T.p8[:, :], T.hl[:, 0:256], F.Identity, bias=2304.0, scale=768.0))
+    to = sig(V.tensor_tensor(T.o16[:, :], T.ax[:, 0:256], ps[3][:, 0:256], A.max))
+    second(1)
     w("p", z1h, to)
     for k in range(16):
         m = mm(ps[5][:, 0:16], T.z1[:, 15 - k:143 - k], T.o16[:, k:256:16], k == 0, k == 15)
     m_o = sig(m)
     mm(ps[4][:, 0:256], cz(FT), T.fl[:, 8:264], True, False)
     m_p = sig(mm(ps[4][:, 0:256], cz(DG), T.fl[:, 8:264], False, True))
-    w("v", c_p5)
-    hlc = new()
-    for hh in range(2):
-        sig(V.tensor_tensor(T.hl[:, 256 + 128 * hh:384 + 128 * hh], ps[6 + hh][:, 0:128], T.p5[:, 128 * hh:128 * hh + 128],
-                            A.subtract), hlc)
-    zxh = sig(V.tensor_copy(T.zx[:, :], cz(ZX, 144)))
-    sig(V.tensor_copy(T.nmb[:, 256:512], T.onl[:, :]), nm1)
-    w("g", hlp, hlc)
+    w("p", x1, hlc)
+    mm(ps[0][:, 0:256], cz(I256), T.hl[:, 0:256], True, False)
+    m_cp = sig(mm(ps[0][:, 0:256], cz(I1), T.hl[:, 256:512], False, True))
+    w("s", m_cp)
+    tcd = sig(S.activation(T.cd[:, :], ps[0][:, 0:256], F.Identity, bias=-2304.0 - BW))
+    w("g", x1, hlc)
     send(d1, T.lhl1[:, :], T.hl[:, :], "lhl1_s")
     send(d2, T.lhl2[:, :], T.hl[:, :], "lhl2_s")
+    cu = new()
+    sig(V.tensor_scalar(T.colU[:, :], T.p16[:, :], 256.0, None, A.mult), cu)
+    w("v", n128)
+    sig(V.tensor_tensor(T.nmb[:, 256:512], T.own_i[:, :], ps[1][:, 0:256], A.subtract), nm1)
+    w("s", nm1, t_sc)
+    dsig(S.dma_start(T.dat[4:128:16, :], T.nmb[:, 0:256]), tab0)
+    dsig(S.dma_start(T.dat[5:128:16, :], T.nmb[:, 256:512]), tab0)
     w("v", m_o)
     tol = sig(V.tensor_copy(T.ol[:, :], ps[5][:, 0:16]))
     w("v", tol, t_mk, k5)
@@ -315,114 +345,111 @@ def rank_program(g, core, T, topo):
     for k in range(16):
         mm(ps[2][:, 0:64], cz(Z1 + 15 - k), T.cm[:, k:1024:16], k == 0, False)
     w("v", m_p)
-    twq = sig(V.tensor_tensor(T.wq[:, :], T.ax[:, :], ps[4][:, 0:256], A.add))
-    w("v", c_p8)
-    tcd = new()
-    for hh in range(2):
-        sig(V.tensor_tensor(T.cd[:, 128 * hh:128 * hh + 128], ps[6 + hh][:, 0:128], T.p8[:, 128 * hh:128 * hh + 128],
-                            A.subtract), tcd)
+    twq = sig(V.tensor_tensor(T.wq[:, :], T.ax[:, 0:256], ps[4][:, 0:256], A.add))
+    w("v", k4)
+    zxh = sig(V.tensor_copy(T.zx[:, :], cz(ZX, 144)))
     w("v", m_l1)
     tl1 = sig(V.tensor_copy(T.l1[:, :], ps[5][:, 64:128]))
-    w("v", tl1, twq, k6)
+    w("v", tl1, twq, km)
     tse = sig(V.tensor_tensor(T.sel[:, :], T.wq[:, :].indirect(T.l1[:, :]), T.mrow[:, :], A.is_equal))
-    w("s", nm1, t_tb)
-    dsig(S.dma_start(T.tb1[4:128:16, 16:4112], T.nmb[:, 0:256]), tab1)
-    dsig(S.dma_start(T.tb1[5:128:16, 16:4112], T.nmb[:, 256:512]), tab1)
-    for tb, ld, sm, src, tk in ((T.tb1, T.lhl1, "lhl1_s", s1, tab1), (T.tb2, T.lhl2, "lhl2_s", s2, tab2)):
+    for tb, ld, sm, src, tok in ((T.tb1, T.lhl1, "lhl1_s", s1, tab1), (T.tb2, T.lhl2, "lhl2_s", s2, tab2)):
         landed("y", sm, src)
         for s_ in range(2):
-            dsig(Y.dma_start(tb[s_:128:16, 16:4112], ld[:, 256 * s_:256 * s_ + 256]), tk)
+            dsig(Y.dma_start(tb[s_:128:16, 16:4112], ld[:, 256 * s_:256 * s_ + 256]), tok)
 
     w("s", k4, cu)
-    ksc, fw = new(), new()
-    sig(S.activation(view(ZL, 15), vx, F.Copy, scale=4096.0), ksc)
+    ksc, fw, ttm, cv = new(), new(), new(), new()
     sig(S.activation(view(ZU, 15), vx, F.Copy, scale=T.colU[:, :]), ksc)
-    sig(S.activation(T.win[:, 0:264], T.zb[:, 0:264], F.Identity, bias=T.colF[:, :]), fw)
     w("p", tse, ksc)
     for k in range(16):
         m = mm(ps[2][:, 0:64], cz(ZU + 15 - k), T.sel[:, k:1024:16], False, k == 15)
     m_lo = sig(m)
-    for k in range(16):
-        mm(ps[5][:, 128:192], cz(ZL + 15 - k), T.sel[:, k:1024:16], k == 0, False)
     w("v", tse, tcd)
     ths = sig(V.tensor_tensor(T.hls[:, :], T.cd[:, :].indirect(T.l1[:, :]), T.sel[:, :], A.mult))
     w("p", ths, zxh)
     for k in range(16):
-        m = mm(ps[5][:, 128:192], T.zx[:, 15 - k:143 - k], T.hls[:, k:1024:16], False, k == 15)
+        m = mm(ps[5][:, 128:192], T.zx[:, 15 - k:143 - k], T.hls[:, k:1024:16], k == 0, k == 15)
     m_l2 = sig(m)
-    tll = new()
+    tll0, tll = new(), new()
     w("v", m_lo)
-    sig(V.tensor_scalar(T.ll[:, 64:128], ps[2][:, 0:64], 16.0, None, A.add), tll)
-    w("v", m_l2)
-    sig(V.tensor_scalar(T.ll[:, 0:64], ps[5][:, 128:192], -2033.0, None, A.add), tll)
+    sig(V.tensor_copy(T.ll[:, 64:128], ps[2][:, 0:64]), tll0)
+    sig(V.tensor_scalar(T.colN[:, :], T.p16[:, :], -1.0, None, A.mult), cv)
+    sig(V.tensor_scalar(T.colF[:, :], T.p16[:, :], 8, -1.0, A.is_equal, A.mult), cv)
 
-    def pick(tb, lst, at, cut, out, toks):
-        ts = []
-        for q, u, v in (("v", 0, cut), ("s", cut, 64)):
-            w(q, *toks)
-            src, o = tb[:, :].indirect(lst[:, at + u:at + v]), out[:, 16 * u:16 * v]
-            ts.append(sig(V.tensor_copy(o, src) if q == "v" else S.activation(o, src, F.Copy)))
-        return ts
-    tr1 = pick(T.tb1, T.ll, 0, 32, T.r1, [tll, tab1])
-    tng = pick(T.tb1, T.ll, 64, NG, T.ng, [tll])
-    w("p", tcd, tll, *tr1)
+    def pick(q, tb, lst, at, u, v, out, tok, *toks):
+        w(q, *toks)
+        src, o = tb[:, :].indirect(lst[:, at + u:at + v]), out[:, 16 * u:16 * v]
+        sig(V.tensor_copy(o, src) if q == "v" else S.activation(o, src, F.Copy), tok)
+    tng, tr1, tr2 = new(), new(), new()
+    pick("s", T.dat, T.ll, 64, 0, N0, T.ng, tng, tll0, tab0)
+    w("v", m_l2)
+    sig(V.tensor_scalar(T.ll[:, 0:64], ps[5][:, 128:192], 2063.0, None, A.add), tll)
+    pick("v", T.tb1, T.ll, 0, 0, R1, T.r1, tr1, tll, tab1)
+    pick("s", T.tb1, T.ll, 0, R1, 64, T.r1, tr1, tll, tab1)
+    pick("v", T.dat, T.ll, 64, N0, N1, T.ng, tng, tll0, tab0)
+    pick("s", T.dat, T.ll, 64, N1, 64, T.ng, tng, tll0, tab0)
+    w("p", tcd, nm1, tll, tr1)
     for k in range(16):
         m = mm(ps[1][:, 0:64], cz(ZW + 15 - k), T.r1[:, k:1024:16], k == 0, k == 15)
     m_l3 = sig(m)
-    for hh in range(2):
-        mm(ps[6 + hh][:, :], cz(FP), T.r1[:, 512 * hh:512 * hh + 512], True, False)
+    w("p", hlc, tng)
+    mm(ps[6][:, :], cz(FN), T.ng[:, 0:512], True, False)
+    m_ac = sig(mm(ps[6][:, :], cz(FP), T.r1[:, 0:512], False, True))
+    w("s", ta, cv)
+    sig(S.activation(T.totm[:, :], T.ax[:, 256:257], F.Identity, bias=T.colN[:, :]), ttm)
+    sig(S.activation(T.win[:, 0:264], T.zb[:, 0:264], F.Identity, bias=T.colF[:, :]), fw)
     w("v", m_l3)
-    tl3 = sig(V.tensor_scalar(T.l3[:, :], ps[1][:, 0:64], -241.0, None, A.add))
-    tr2 = pick(T.tb2, T.l3, 0, 32, T.r2, [tl3, tab2])
-    w("p", *tng)
-    for hh in range(2):
-        mm(ps[6 + hh][:, :], cz(FN), T.ng[:, 512 * hh:512 * hh + 512], False, False)
-    w("p", *tr2)
+    tl3 = sig(V.tensor_scalar(T.l3[:, :], ps[1][:, 0:64], -241.0 - BW, None, A.add))
+    pick("v", T.tb2, T.l3, 0, 0, R2, T.r2, tr2, tl3, tab2)
+    pick("s", T.tb2, T.l3, 0, R2, 64, T.r2, tr2, tl3, tab2)
+    w("v", ttm, ks)
+    ttk = sig(V.tensor_scalar(T.tk[:, :], T.sl[:, :], T.totm[:, :], None, A.is_ge))
+    w("s", ttk)
+    tth = sig(S.activation(T.thr[:, :], T.tk[:, :], F.Copy, bias=BW, scale=8192.0))
+    w("p", tr2)
     for k in range(16):
         m = mm(ps[0][:, 256:320], cz(ZW + 15 - k), T.r2[:, k:1024:16], k == 0, k == 15)
     m_l4 = sig(m)
-    for hh in range(2):
-        mm(ps[6 + hh][:, :], cz(FP), T.r2[:, 512 * hh:512 * hh + 512], False, False)
+    w("v", m_ac, tr2)
+    tfd = [sig(V.tensor_tensor(T.fd[:, 0:512], ps[6][:, :], T.r2[:, 0:512], A.add))]
 
     w("v", m_l4)
-    tl5 = sig(V.tensor_scalar(T.l5[:, :], ps[0][:, 256:320], -241.0, None, A.add))
+    tl5 = sig(V.tensor_scalar(T.l5[:, :], ps[0][:, 256:320], -241.0 - BW, None, A.add))
+    w("v", tth)
+    f4 = sig(V.tensor_tensor(T.fl4[:, 8:72], ps[0][:, 256:320], T.thr[:, :], A.is_gt))
+    x2 = sig(V.tensor_tensor(T.xn[:, :], ps[0][:, 256:320], T.thr[:, :], A.is_le))
     w("s", tl5)
     tr3 = [sig(S.activation(T.r3[:, 512 * hh:512 * hh + 512], T.tb1[:, :].indirect(T.l5[:, 32 * hh:32 * hh + 32]), F.Copy))
            for hh in range(2)]
-    f4 = sig(V.tensor_scalar(T.fl4[:, 8:72], ps[0][:, 256:320], 0.0, None, A.is_gt))
-    x2 = sig(V.tensor_scalar(T.xn[:, :], ps[0][:, 256:320], 0.0, -4096.0, A.is_gt, A.mult))
+    mm(ps[7][:, :], cz(FN), T.ng[:, 512:1024], True, False)
     w("p", f4, zz)
-    m_a = sig(mm(ps[2][:, 0:64], cz(FO), T.fl4[:, 7:71], True, True))
-    m_q = sig(mm(ps[3][:, 0:64], cz(FT), T.fl4[:, 8:72], True, True))
-    m_fd = []
-    for hh in range(2):
-        w("p", tr3[hh])
-        m_fd.append(sig(mm(ps[6 + hh][:, :], cz(FQ), T.r3[:, 512 * hh:512 * hh + 512], False, True)))
+    mm(ps[2][:, 0:64], cz(FS), T.fl4[:, 7:71], True, False)
+    m_a = sig(mm(ps[2][:, 0:64], cz(FT), T.fl4[:, 8:72], False, True))
+    mm(ps[7][:, :], cz(FP), T.r1[:, 512:1024], False, False)
+    m_ad = sig(mm(ps[7][:, :], cz(FR), T.r2[:, 512:1024], False, True))
+    w("s", m_ad)
+    tfd.append(sig(S.activation(T.fd[:, 512:1024], ps[7][:, :], F.Copy)))
     w("v", x2, k6)
-    x3 = sig(V.tensor_tensor(T.xx[:, :], T.xn[:, :], T.rw[:, :], A.add))
+    x3 = sig(V.tensor_tensor(T.xx[:, :], T.xn[:, :], T.rw[:, :], A.mult))
     w("v", m_a)
     q1 = sig(V.tensor_tensor_scan(T.a4[:, :], ps[2][:, 0:64], T.zb[:, 0:64], 0.0, A.add, A.add))
-    w("v", q1, m_q)
-    q2 = sig(V.tensor_tensor(T.q4[:, :], T.a4[:, :], ps[3][:, 0:64], A.add))
-    w("v", q2, x3)
-    q3 = sig(V.tensor_tensor(T.o4[:, :], T.q4[:, :], T.xx[:, :], A.max))
+    w("v", q1, x3)
+    q3 = sig(V.tensor_tensor(T.o4[:, :], T.a4[:, :], T.xx[:, :], A.max))
     w("v", q3)
     q5 = sig(V.tensor_copy(T.l4[:, :], T.o4[:, :]))
-    w("v", m_fd[0])
-    w("s", m_fd[1])
-    tfd = [sig(V.tensor_copy(T.fd[:, 0:512], ps[6][:, :])), sig(S.activation(T.fd[:, 512:1024], ps[7][:, :], F.Copy))]
     w("v", q5, fw)
     tw = None
     for hh in range(2):
-        w("v", tfd[hh])
+        w("v", tfd[hh], tr3[hh])
         if tw:
             w("v", tw)
-        tw = sig(V.tensor_copy(T.win[:, :].indirect(T.l4[:, 32 * hh:32 * hh + 32]), T.fd[:, 512 * hh:512 * hh + 512]))
+        tw = sig(V.tensor_tensor(T.win[:, :].indirect(T.l4[:, 32 * hh:32 * hh + 32]), T.fd[:, 512 * hh:512 * hh + 512],
+                                 T.r3[:, 512 * hh:512 * hh + 512], A.add))
     w("y", tw)
     t_y = new()
     w("s", tw)
-    dsig(Y.dma_start(T.yk[:, :], T.win[0:128:16, 1:257]), t_y)
-    dsig(S.dma_start(T.ys[:, :], T.win[1:128:16, 1:257]), t_y)
+    dsig(Y.dma_start(T.yk[:, :], T.win[8:128:16, 1:257]), t_y)
+    dsig(S.dma_start(T.ys[:, :], T.win[9:128:16, 1:257]), t_y)
     for t in made:
         if waited.get(t[0], 0) < t[1]:
             w("y", t)

from concourse.mybir import AluOpType as A, ActivationFunctionType as F

BF, F32, F16, I32, U16 = "bfloat16", "float32", "float16", "int32", "uint16"
SCRATCH = {
    "own_i": ("sbuf", [128, 256], I32), "nxt_i": ("sbuf", [128, 256], I32), "pts_i": ("sbuf", [128, 256], I32),
    "own_u": ("sbuf", [128, 256], U16), "nxt_u": ("sbuf", [128, 256], U16), "own_r": ("sbuf", [128, 256], U16),
    "onh": ("sbuf", [128, 256], BF), "nmb": ("sbuf", [128, 512], BF),
    "ptsb": ("sbuf", [128, 256], BF), "zb": ("sbuf", [128, 1028], BF),
    "tab": ("sbuf", [128, 16384], BF), "dat": ("sbuf", [128, 4096], BF), "gat": ("sbuf", [128, 4096], BF),
    "pidx": ("sbuf", [128, 1], I32), "par": ("sbuf", [128, 1], I32), "p16": ("sbuf", [128, 1], I32),
    "colA": ("sbuf", [128, 1], F32), "colB": ("sbuf", [128, 1], F32), "colF": ("sbuf", [128, 1], F32),
    "colU": ("sbuf", [128, 1], F32), "colN": ("sbuf", [128, 1], F32), "totm": ("sbuf", [128, 1], F32),
    "lb0": ("sbuf", [128, 16], F32), "lb": ("sbuf", [128, 16], F32),
    "bl": ("sbuf", [128, 256], BF), "bh": ("sbuf", [128, 256], BF), "bx": ("sbuf", [128, 256], BF),
    "by": ("sbuf", [128, 256], BF), "bs": ("sbuf", [128, 256], BF),
    "cz": ("sbuf", [128, 2176], BF),
    "z1": ("sbuf", [128, 144], F16), "zx": ("sbuf", [128, 144], F16), "t32": ("sbuf", [1, 256], BF),
    "c32": ("sbuf", [1, 256], BF),
    "mrow": ("sbuf", [128, 1024], F32), "cio": ("sbuf", [128, 256], BF), "rw": ("sbuf", [128, 64], F32),
    "sl": ("sbuf", [128, 64], F32), "tk": ("sbuf", [128, 64], F32), "thr": ("sbuf", [128, 64], F32),
    "mk": ("sbuf", [128, 1280], BF), "pr8": ("sbuf", [8, 4096], BF), "pt": ("sbuf", [128, 256], BF),
    "ng": ("sbuf", [128, 1024], BF), "hl": ("sbuf", [128, 512], BF),
    "p5": ("sbuf", [128, 256], F32), "cd": ("sbuf", [128, 256], F32),
    "fl": ("sbuf", [128, 264], BF),
    "ax": ("sbuf", [128, 257], F32), "o16": ("sbuf", [128, 256], F16), "wq": ("sbuf", [128, 256], F32),
    "ol": ("sbuf", [128, 16], U16), "cm": ("sbuf", [128, 1024], BF), "l1": ("sbuf", [128, 64], U16),
    "sel": ("sbuf", [128, 1024], BF), "hls": ("sbuf", [128, 1024], F16),
    "ll": ("sbuf", [128, 128], U16), "l3": ("sbuf", [128, 64], U16), "l4": ("sbuf", [128, 64], U16),
    "l5": ("sbuf", [128, 64], U16),
    "tb1": ("sbuf", [128, 4112], BF), "tb2": ("sbuf", [128, 4112], BF),
    "r1": ("sbuf", [128, 1024], BF), "r2": ("sbuf", [128, 1024], BF), "r3": ("sbuf", [128, 1024], F32),
    "fl4": ("sbuf", [128, 72], BF), "xn": ("sbuf", [128, 64], F32), "xx": ("sbuf", [128, 64], F32),
    "a4": ("sbuf", [128, 64], F32), "o4": ("sbuf", [128, 64], F32),
    "fd": ("sbuf", [128, 1024], F32), "win": ("sbuf", [128, 1408], F32),
    "lpt1": ("dram", [128, 256], BF), "lpt2": ("dram", [128, 256], BF), "lpt3": ("dram", [128, 256], BF),
    "lhl1": ("dram", [128, 512], BF), "lhl2": ("dram", [128, 512], BF),
}
for _b in range(8):
    SCRATCH["ps%d" % _b] = ("psum", [128, 512], F32)
NE = 138
SEMAPHORES = ["own_r_s", "lpt1_s", "lpt2_s", "lpt3_s", "lhl1_s", "lhl2_s", "ls"] + ["e%d" % _i for _i in range(NE)]

I1, I256 = 0, 2048
ZW, ZN, EP, Z1, ZX, ZU = 144, 288, 432, 576, 720, 864
FS, ON4, DG, FO, FT, FP, FN, FR = 1024, 1152, 1280, 1408, 1536, 1664, 1792, 1920
TG0, TG, TD, TS = 384, 1408, 2048, 6656
AE = 1536
N0, N1, R1, R2 = 20, 36, 36, 36
B0 = 192.0
BW = 256.0 * B0


def rank_program(g, core, T, topo):
    r = T.rank_of(core)
    if r is None:
        return
    n = len(T.cores)
    d1, d2, d3 = (T.cores[(r - k) % n] for k in (1, 2, 3))
    s1, s2, s3 = (T.cores[(r + k) % n] for k in (1, 2, 3))
    V, S, P, Y = g.vector, g.scalar, g.tensor, g.sync
    Q = {"g": g, "v": V, "s": S, "p": P, "y": Y}
    ctr, seen, waited, made, ls = [0], {}, {}, [], [0]

    def new():
        t = ["e%d" % ctr[0], 0]
        ctr[0] += 1
        made.append(t)
        return t

    def sig(ins, t=None, by=1):
        t = t or new()
        ins.then_inc(T.sem[t[0]], by)
        t[1] += by
        return t

    def dsig(ins, t=None):
        return sig(ins, t, 16)

    def w(q, *toks):
        for t in toks:
            if seen.get((q, t[0]), 0) < t[1]:
                Q[q].wait_ge(T.sem[t[0]], t[1])
                seen[(q, t[0])] = t[1]
                waited[t[0]] = t[1]

    def landed(q, nm, src):
        Q[q].wait_ge(T.sem[nm], len(topo.engines(src, core)))

    def send(dst, out, in_, sem):
        rid, pid = topo.addr(dst)[:2]
        eng = topo.engines(core, dst)
        g.remote_dma(out_ap=out, in_ap=in_, remote_sem=T.sem[sem], local_sem=T.sem.ls, pid=pid, routing_id=rid,
                     dma_engine_mask=sum(1 << e for e in eng))
        ls[0] += len(eng)

    def iota(out, pattern, base=0, cm=0):
        return g.iota(out, pattern, base, cm, allow_small_or_imprecise_dtypes=True)

    def cz(b, width=128, rows=128):
        return T.cz[0:rows, b:b + width]

    def mm(out, lhsT, rhs, first, last):
        return P.matmul(out, lhsT, rhs, first, last)

    ps = [T["ps%d" % b] for b in range(8)]

    t_own = dsig(Y.dma_start(T.own_i[:, :], T.own[:, :]))
    t_nxt = dsig(S.dma_start(T.nxt_i[:, :], T.nxt[:, :]))
    t_pts = dsig(Y.dma_start(T.pts_i[:, :], T.pts[:, :]))

    k0, k1, k5 = new(), new(), new()
    f_tab, f_tabv, t_tab, t_cz = new(), new(), new(), new()
    sig(g.iota(T.pidx[:, :], [[0, 1]], 0, 1), k0)
    sig(iota(T.lb0[:, :], [[16, 16]]), k0)
    sig(iota(T.bl[:, :], [[1, 16], [0, 16]]), k1)
    sig(iota(T.bh[:, :], [[0, 16], [1, 16]]), k1)
    sig(iota(T.tab[:, 0:TG0], [[0, TG0]]), f_tab)

    z0 = sig(V.memset(T.zb[:, :], 0.0))
    w("s", z0)
    for a in range(TG + TD, TG + TD + TS, 1024):
        b = min(a + 1024, TG + TD + TS)
        sig(S.activation(T.tab[:, a:b], T.zb[:, 0:b - a], F.Copy), f_tab)
    w("y", z0)
    for a in range(TG, TG + TD, 1024):
        dsig(Y.dma_start(T.tab[:, a:a + 1024], T.zb[:, 0:1024]), t_tab)
    for a in (0, 1024):
        dsig(Y.dma_start(T.cz[:, a:a + 1024], T.zb[:, 0:1024]), t_cz)
    V0 = TG + TD + TS
    VE = V0 + 2048
    sig(V.memset(T.tab[:, V0:VE], 0.0), f_tabv)

    w("v", k0)
    c1, cc = new(), new()
    sig(V.tensor_scalar(T.par[:, :], T.pidx[:, :], 1, None, A.bitwise_and), c1)
    sig(V.tensor_scalar(T.p16[:, :], T.pidx[:, :], 15, None, A.bitwise_and), c1)
    w("v", c1)
    sig(V.tensor_copy(T.colB[:, :], T.par[:, :]), cc)
    sig(V.tensor_scalar(T.colA[:, :], T.par[:, :], 0, None, A.is_equal), cc)
    w("v", cc, k1)
    b1 = new()
    sig(V.tensor_scalar(T.lb[:, :], T.lb0[:, :], T.colB[:, :], None, A.mult), b1)
    sig(V.tensor_scalar(T.bx[:, :], T.bl[:, :], T.colB[:, :], 1.0, A.mult, A.add), b1)
    sig(V.tensor_scalar(T.by[:, :], T.bh[:, :], T.colA[:, :], None, A.mult), b1)
    w("v", t_own)
    c_own = sig(V.tensor_copy(T.own_u[:, :], T.own_i[:, :]))
    w("v", b1)
    b2 = sig(V.tensor_tensor(T.bs[:, :], T.bx[:, :], T.by[:, :], A.add))
    w("v", b2)
    da, db = new(), new()
    for ch in range(AE // 256):
        sig(V.tensor_scalar(T.dat[:, 256 * ch:256 * ch + 256], T.bs[:, :], T.lb[:, ch:ch + 1], None, A.add), da)
    w("v", t_pts)
    c_pts = sig(V.tensor_copy(T.ptsb[:, :], T.pts_i[:, :]))
    w("v", t_nxt)
    c_nxt = sig(V.tensor_copy(T.nxt_u[:, :], T.nxt_i[:, :]))
    sig(V.memset(T.tab[:, VE:16384], 0.0), f_tabv)
    w("s", b1, b2)
    for ch in range(AE // 256, 16):
        sig(S.activation(T.dat[:, 256 * ch:256 * ch + 256], T.bs[:, :], F.Identity, bias=T.lb[:, ch:ch + 1]), db)

    w("g", c_own)
    send(d1, T.own_r[:, :], T.own_u[:, :], "own_r_s")
    sig(iota(T.tab[:, TG0:TG], [[0, TG - TG0]]), f_tab)
    sig(iota(T.cio[:, :], [[1, 256]]), k5)
    k6, km, ks, zz = new(), new(), new(), new()
    sig(iota(T.mrow[:, 0:128], [[1, 128]], 2049), km)
    sig(iota(T.rw[:, :], [[16, 64]], 264, 1), k6)

    w("v", f_tab, f_tabv, t_tab, da)
    landed("v", "own_r_s", s1)
    t_s0 = sig(V.tensor_copy(T.tab[:, :].indirect(T.own_r[:, 0:AE // 16]), T.dat[:, 0:AE]))
    w("v", db, t_s0)
    t_sc = sig(V.tensor_copy(T.tab[:, :].indirect(T.own_r[:, AE // 16:256]), T.dat[:, AE:4096]))

    w("y", c_pts)
    t_pr8 = dsig(Y.dma_start(T.pr8[:, :], T.ptsb[:, :]))
    t_tb = new()
    for tb in (T.tb1, T.tb2):
        for a in range(0, 4112, 1028):
            dsig(Y.dma_start(tb[:, a:a + 1028], T.zb[:, :]), t_tb)

    def view(b, start):
        return T.cz[:, b + start:b + start + 113:16]

    def put(x, part, wt):
        return g.affine_select(x, x, [[-16, 8]], A.not_equal, wt, -part, 1)

    def setw(x, pattern, wt, base, cm):
        return g.affine_select(x, x, pattern, A.is_ge, wt, base, cm)
    k2, k3, k4, kf, kz = new(), new(), new(), new(), new()
    ep = T.cz[0:8, EP + 15:EP + 128:16]
    grp = [[16, 8], [0, 16]]
    vx = view(ZX, 15)
    w("g", t_cz)
    sig(g.affine_select(ep, ep, [[-1, 8]], A.not_equal, 1.0, 0, 1), k2)
    sig(put(view(ZN, 15), 0, 1024.0), kz)
    w("g", kz)
    sig(put(view(ZN, 15), 1, 1.0), kz)
    sig(setw(cz(FO), grp, 1.0, -1, -1), kf)
    w("g", kf)
    sig(setw(cz(FO), grp, 0.0, 15, -1), kf)
    sig(put(view(Z1, 15), 0, 1.0), k3)
    sig(setw(vx, [[16, 8]], 1.0, -1, -1), k3)
    sig(put(view(ZW, 15), 0, 256.0), k3)
    sig(put(view(FN, 8), 4, 128.0), k3)
    w("g", kf)
    sig(g.affine_select(cz(FT), cz(FO), [[1, 128]], A.is_ge, 0.0, 0, -1), k4)
    sig(g.affine_select(cz(FS), cz(FO), [[-1, 128]], A.is_gt, 0.0, 0, 1), k4)
    ki = sig(g.affine_select(cz(I1), cz(I1), [[-1, 128]], A.not_equal, 1.0, 0, 1))
    sig(put(view(FP, 9), 2, 1.0), k4)
    sig(put(view(FR, 9), 9, 1.0), k4)
    sig(put(view(FN, 9), 6, 1.0), k4)
    w("g", k3)
    sig(setw(vx, [[16, 8]], 0.0, 15, -1), k4)
    sig(put(view(ZW, 15), 1, 1.0), k4)
    sig(put(view(FN, 8), 5, 1.0), k4)

    kr = new()
    sig(S.activation(T.t32[:, :], T.zb[0:1, 0:256], F.Identity, bias=32.0), kr)
    sig(S.activation(T.fl[:, 0:8], T.zb[:, 0:8], F.Copy), zz)
    sig(S.activation(T.fl4[:, 0:8], T.zb[:, 0:8], F.Copy), zz)
    w("s", k5)
    sig(S.activation(T.c32[:, :], T.cio[0:1, :], F.Copy, scale=1.0 / 32), kr)
    for b in (128, 256, 512):
        w("s", km)
        sig(S.activation(T.mrow[:, b:2 * b], T.mrow[:, 0:b], F.Identity, bias=float(b)), km)
    w("s", km)
    sig(S.activation(T.sl[:, :], T.mrow[:, 0:1024:16], F.Identity, bias=-2049.0), ks)
    w("p", t_pr8, k2)
    for kk in range(16):
        m = mm(ps[2][:, 0:256], cz(EP + 15 - kk, 128, 8), T.pr8[:, kk:4096:16], kk == 0, kk == 15)
    m_pt = sig(m)
    w("s", m_pt)
    c_pt = sig(S.activation(T.pt[:, :], ps[2][:, 0:256], F.Copy))
    w("s", kf)
    sig(S.activation(cz(ON4), cz(FO), F.Copy, scale=-2048.0), kr)
    w("s", ki)
    sig(S.activation(cz(DG), cz(I1), F.Copy, scale=2048.0), kr)
    sig(S.activation(cz(I256), cz(I1), F.Copy, scale=256.0), kr)
    w("g", c_pt)
    send(d1, T.lpt1[:, :], T.pt[:, :], "lpt1_s")
    send(d2, T.lpt2[:, :], T.pt[:, :], "lpt2_s")
    send(d3, T.lpt3[:, :], T.pt[:, :], "lpt3_s")
    t_mk = sig(iota(T.mk[:, 0:1024], [[0, 1024]]))
    tab0, tab1, tab2 = new(), new(), new()
    w("y", c_pt, t_sc)
    dsig(Y.dma_start(T.dat[6:128:16, :], T.pt[:, :]), tab0)
    w("y", t_tb)
    landed("y", "lpt1_s", s1)
    dsig(Y.dma_start(T.tb1[2:128:16, 16:4112], T.lpt1[:, :]), tab1)
    landed("y", "lpt2_s", s2)
    dsig(Y.dma_start(T.tb2[9:128:16, 16:4112], T.lpt2[:, :]), tab2)
    landed("y", "lpt3_s", s3)
    dsig(Y.dma_start(T.tb1[9:128:16, 16:4112], T.lpt3[:, :]), tab1)

    w("s", t_sc, c_nxt)
    w("v", t_sc, c_nxt)
    gt = []
    for j in range(4):
        t = new()
        for hh in range(2):
            a = 1024 * j + 512 * hh
            o, src = T.gat[:, a:a + 512], T.tab[:, :].indirect(T.nxt_u[:, a // 16:a // 16 + 32])
            sig(S.activation(o, src, F.Copy) if hh else V.tensor_copy(o, src), t)
        gt.append(t)
    m_cd = [new(), new()]
    w("p", kr)
    mm(ps[3][:, 0:256], T.t32[:, 0:128], T.t32[:, :], True, False)
    mm(ps[3][:, 0:256], T.t32[:, 0:128], T.c32[:, :], False, False)
    w("p", kz)
    for j in range(4):
        w("p", gt[j])
        for kk in range(16):
            m = mm(ps[6 + j // 2][:, 64 * (j % 2):64 * (j % 2) + 64], cz(ZN + 15 - kk),
                   T.gat[:, 1024 * j + kk:1024 * j + 1024:16], kk == 0, kk == 15)
        sig(m, m_cd[j // 2])

    w("v", m_cd[0])
    f_l, f_l0 = new(), new()
    sig(V.tensor_scalar(T.fl[:, 8:136], ps[6][:, 0:128], 0.0, None, A.is_gt), f_l0)
    hlc, x1, c_p5, nm1 = new(), new(), new(), new()
    nm0 = sig(V.tensor_scalar(T.onh[:, :], T.own_i[:, :], 1.0 / 128, 128.0, A.mult, A.add))

    def first(hh, fl_):
        w("s", m_cd[hh], fl_)
        x = sig(S.activation(T.hl[:, 128 * hh:128 * hh + 128], ps[6 + hh][:, 0:128], F.Identity, bias=B0, scale=1.0 / 1024), x1)
        w("s", x)
        sig(S.activation(T.p5[:, 128 * hh:128 * hh + 128], T.hl[:, 128 * hh:128 * hh + 128], F.Identity, bias=-1024.0 * B0,
                         scale=1024.0), c_p5)

    def second(hh):
        w("v", c_p5)
        sig(V.tensor_tensor(T.hl[:, 256 + 128 * hh:384 + 128 * hh], ps[6 + hh][:, 0:128], T.p5[:, 128 * hh:128 * hh + 128],
                            A.subtract), hlc)
    first(0, f_l0)
    second(0)
    w("s", nm0)
    n128 = sig(S.activation(ps[1][:, 0:256], T.onh[:, :], F.Identity, bias=-16384.0, scale=128.0))
    w("v", m_cd[1])
    sig(V.tensor_scalar(T.fl[:, 136:264], ps[7][:, 0:128], 0.0, None, A.is_gt), f_l)
    w("v", k3)
    z1h = sig(V.tensor_copy(T.z1[:, :], cz(Z1, 144)))
    first(1, f_l)
    sig(S.activation(T.nmb[:, 0:256], T.onh[:, :], F.Identity, bias=-128.0), nm1)
    w("p", f_l0, f_l, zz, c_pt, kf, k3, k4)
    m_c = sig(mm(ps[2][:, 0:257], cz(FO), T.fl[:, 7:264], True, True))
    m_x = sig(mm(ps[3][:, 0:256], cz(ON4), T.fl[:, 8:264], False, True))
    w("v", m_c, z0)
    ta = sig(V.tensor_tensor_scan(T.ax[:, :], ps[2][:, 0:257], T.zb[:, 0:257], 0.0, A.add, A.add))
    w("v", ta, m_x)
    to = sig(V.tensor_tensor(T.o16[:, :], T.ax[:, 0:256], ps[3][:, 0:256], A.max))
    second(1)
    w("p", z1h, to)
    for k in range(16):
        m = mm(ps[5][:, 0:16], T.z1[:, 15 - k:143 - k], T.o16[:, k:256:16], k == 0, k == 15)
    m_o = sig(m)
    mm(ps[4][:, 0:256], cz(FT), T.fl[:, 8:264], True, False)
    m_p = sig(mm(ps[4][:, 0:256], cz(DG), T.fl[:, 8:264], False, True))
    w("p", x1, hlc)
    mm(ps[0][:, 0:256], cz(I256), T.hl[:, 0:256], True, False)
    m_cp = sig(mm(ps[0][:, 0:256], cz(I1), T.hl[:, 256:512], False, True))
    w("s", m_cp)
    tcd = sig(S.activation(T.cd[:, :], ps[0][:, 0:256], F.Identity, bias=-2304.0 - BW))
    w("g", x1, hlc)
    send(d1, T.lhl1[:, :], T.hl[:, :], "lhl1_s")
    send(d2, T.lhl2[:, :], T.hl[:, :], "lhl2_s")
    cu = new()
    sig(V.tensor_scalar(T.colU[:, :], T.p16[:, :], 256.0, None, A.mult), cu)
    w("v", n128)
    sig(V.tensor_tensor(T.nmb[:, 256:512], T.own_i[:, :], ps[1][:, 0:256], A.subtract), nm1)
    w("s", nm1, t_sc)
    dsig(S.dma_start(T.dat[4:128:16, :], T.nmb[:, 0:256]), tab0)
    dsig(S.dma_start(T.dat[5:128:16, :], T.nmb[:, 256:512]), tab0)
    w("v", m_o)
    tol = sig(V.tensor_copy(T.ol[:, :], ps[5][:, 0:16]))
    w("v", tol, t_mk, k5)
    tmk = sig(V.tensor_copy(T.mk[:, :].indirect(T.ol[:, :]), T.cio[:, :]))
    w("v", tmk)
    tcm = sig(V.tensor_tensor_scan(T.cm[:, :], T.mk[:, 0:1024], T.zb[:, 0:1024], 0.0, A.max, A.max))
    w("p", tcm)
    for k in range(16):
        m = mm(ps[5][:, 64:128], cz(Z1 + 15 - k), T.cm[:, k:1024:16], k == 0, k == 15)
    m_l1 = sig(m)
    for k in range(16):
        mm(ps[2][:, 0:64], cz(Z1 + 15 - k), T.cm[:, k:1024:16], k == 0, False)
    w("v", m_p)
    twq = sig(V.tensor_tensor(T.wq[:, :], T.ax[:, 0:256], ps[4][:, 0:256], A.add))
    w("v", k4)
    zxh = sig(V.tensor_copy(T.zx[:, :], cz(ZX, 144)))
    w("v", m_l1)
    tl1 = sig(V.tensor_copy(T.l1[:, :], ps[5][:, 64:128]))
    w("v", tl1, twq, km)
    tse = sig(V.tensor_tensor(T.sel[:, :], T.wq[:, :].indirect(T.l1[:, :]), T.mrow[:, :], A.is_equal))
    for tb, ld, sm, src, tok in ((T.tb1, T.lhl1, "lhl1_s", s1, tab1), (T.tb2, T.lhl2, "lhl2_s", s2, tab2)):
        landed("y", sm, src)
        for s_ in range(2):
            dsig(Y.dma_start(tb[s_:128:16, 16:4112], ld[:, 256 * s_:256 * s_ + 256]), tok)

    w("s", k4, cu)
    ksc, fw, ttm, cv = new(), new(), new(), new()
    sig(S.activation(view(ZU, 15), vx, F.Copy, scale=T.colU[:, :]), ksc)
    w("p", tse, ksc)
    for k in range(16):
        m = mm(ps[2][:, 0:64], cz(ZU + 15 - k), T.sel[:, k:1024:16], False, k == 15)
    m_lo = sig(m)
    w("v", tse, tcd)
    ths = sig(V.tensor_tensor(T.hls[:, :], T.cd[:, :].indirect(T.l1[:, :]), T.sel[:, :], A.mult))
    w("p", ths, zxh)
    for k in range(16):
        m = mm(ps[5][:, 128:192], T.zx[:, 15 - k:143 - k], T.hls[:, k:1024:16], k == 0, k == 15)
    m_l2 = sig(m)
    tll0, tll = new(), new()
    w("v", m_lo)
    sig(V.tensor_copy(T.ll[:, 64:128], ps[2][:, 0:64]), tll0)
    sig(V.tensor_scalar(T.colN[:, :], T.p16[:, :], -1.0, None, A.mult), cv)
    sig(V.tensor_scalar(T.colF[:, :], T.p16[:, :], 8, -1.0, A.is_equal, A.mult), cv)

    def pick(q, tb, lst, at, u, v, out, tok, *toks):
        w(q, *toks)
        src, o = tb[:, :].indirect(lst[:, at + u:at + v]), out[:, 16 * u:16 * v]
        sig(V.tensor_copy(o, src) if q == "v" else S.activation(o, src, F.Copy), tok)
    tng, tr1, tr2 = new(), new(), new()
    pick("s", T.dat, T.ll, 64, 0, N0, T.ng, tng, tll0, tab0)
    w("v", m_l2)
    sig(V.tensor_scalar(T.ll[:, 0:64], ps[5][:, 128:192], 2063.0, None, A.add), tll)
    pick("v", T.tb1, T.ll, 0, 0, R1, T.r1, tr1, tll, tab1)
    pick("s", T.tb1, T.ll, 0, R1, 64, T.r1, tr1, tll, tab1)
    pick("v", T.dat, T.ll, 64, N0, N1, T.ng, tng, tll0, tab0)
    pick("s", T.dat, T.ll, 64, N1, 64, T.ng, tng, tll0, tab0)
    w("p", tcd, nm1, tll, tr1)
    for k in range(16):
        m = mm(ps[1][:, 0:64], cz(ZW + 15 - k), T.r1[:, k:1024:16], k == 0, k == 15)
    m_l3 = sig(m)
    w("p", hlc, tng)
    mm(ps[6][:, :], cz(FN), T.ng[:, 0:512], True, False)
    m_ac = sig(mm(ps[6][:, :], cz(FP), T.r1[:, 0:512], False, True))
    w("s", ta, cv)
    sig(S.activation(T.totm[:, :], T.ax[:, 256:257], F.Identity, bias=T.colN[:, :]), ttm)
    sig(S.activation(T.win[:, 0:264], T.zb[:, 0:264], F.Identity, bias=T.colF[:, :]), fw)
    w("v", m_l3)
    tl3 = sig(V.tensor_scalar(T.l3[:, :], ps[1][:, 0:64], -241.0 - BW, None, A.add))
    pick("v", T.tb2, T.l3, 0, 0, R2, T.r2, tr2, tl3, tab2)
    pick("s", T.tb2, T.l3, 0, R2, 64, T.r2, tr2, tl3, tab2)
    w("v", ttm, ks)
    ttk = sig(V.tensor_scalar(T.tk[:, :], T.sl[:, :], T.totm[:, :], None, A.is_ge))
    w("s", ttk)
    tth = sig(S.activation(T.thr[:, :], T.tk[:, :], F.Copy, bias=BW, scale=8192.0))
    w("p", tr2)
    for k in range(16):
        m = mm(ps[0][:, 256:320], cz(ZW + 15 - k), T.r2[:, k:1024:16], k == 0, k == 15)
    m_l4 = sig(m)
    w("v", m_ac, tr2)
    tfd = [sig(V.tensor_tensor(T.fd[:, 0:512], ps[6][:, :], T.r2[:, 0:512], A.add))]

    w("v", m_l4)
    tl5 = sig(V.tensor_scalar(T.l5[:, :], ps[0][:, 256:320], -241.0 - BW, None, A.add))
    w("v", tth)
    f4 = sig(V.tensor_tensor(T.fl4[:, 8:72], ps[0][:, 256:320], T.thr[:, :], A.is_gt))
    x2 = sig(V.tensor_tensor(T.xn[:, :], ps[0][:, 256:320], T.thr[:, :], A.is_le))
    w("s", tl5)
    tr3 = [sig(S.activation(T.r3[:, 512 * hh:512 * hh + 512], T.tb1[:, :].indirect(T.l5[:, 32 * hh:32 * hh + 32]), F.Copy))
           for hh in range(2)]
    mm(ps[7][:, :], cz(FN), T.ng[:, 512:1024], True, False)
    w("p", f4, zz)
    mm(ps[2][:, 0:64], cz(FS), T.fl4[:, 7:71], True, False)
    m_a = sig(mm(ps[2][:, 0:64], cz(FT), T.fl4[:, 8:72], False, True))
    mm(ps[7][:, :], cz(FP), T.r1[:, 512:1024], False, False)
    m_ad = sig(mm(ps[7][:, :], cz(FR), T.r2[:, 512:1024], False, True))
    w("s", m_ad)
    tfd.append(sig(S.activation(T.fd[:, 512:1024], ps[7][:, :], F.Copy)))
    w("v", x2, k6)
    x3 = sig(V.tensor_tensor(T.xx[:, :], T.xn[:, :], T.rw[:, :], A.mult))
    w("v", m_a)
    q1 = sig(V.tensor_tensor_scan(T.a4[:, :], ps[2][:, 0:64], T.zb[:, 0:64], 0.0, A.add, A.add))
    w("v", q1, x3)
    q3 = sig(V.tensor_tensor(T.o4[:, :], T.a4[:, :], T.xx[:, :], A.max))
    w("v", q3)
    q5 = sig(V.tensor_copy(T.l4[:, :], T.o4[:, :]))
    w("v", q5, fw)
    tw = None
    for hh in range(2):
        w("v", tfd[hh], tr3[hh])
        if tw:
            w("v", tw)
        tw = sig(V.tensor_tensor(T.win[:, :].indirect(T.l4[:, 32 * hh:32 * hh + 32]), T.fd[:, 512 * hh:512 * hh + 512],
                                 T.r3[:, 512 * hh:512 * hh + 512], A.add))
    w("y", tw)
    t_y = new()
    w("s", tw)
    dsig(Y.dma_start(T.yk[:, :], T.win[8:128:16, 1:257]), t_y)
    dsig(S.dma_start(T.ys[:, :], T.win[9:128:16, 1:257]), t_y)
    for t in made:
        if waited.get(t[0], 0) < t[1]:
            w("y", t)
    g.wait_ge(T.sem.ls, ls[0])
